import numpy as np
import ml_dtypes


def mxq(x, axis, fmt="e4m3"):
    dtype, down = {"e4m3": (ml_dtypes.float8_e4m3fn, 7), "e5m2": (ml_dtypes.float8_e5m2, 14)}[fmt]
    v = np.moveaxis(np.asarray(x, np.float32).astype(ml_dtypes.bfloat16).astype(np.float64), axis, -1)
    blocks = v.reshape(v.shape[:-1] + (-1, 32))
    amax = np.abs(blocks).max(-1, keepdims=True)
    byte = np.maximum(np.where(amax > 0, np.frexp(amax)[1] - 1 + 127, 0) - down, 1)
    scale = np.exp2(byte - 127.0)
    codes = (blocks / scale).astype(np.float32).astype(dtype).astype(np.float64)
    return np.moveaxis((codes * scale).reshape(v.shape), -1, axis)


WIDE = False


def mx_kscale(k):
    if not WIDE:
        return np.ones(k)
    levels = np.array([10, -10, 5, -5, 0])
    if k % 512:
        return np.exp2(np.random.permutation(np.resize(levels, k // 32))).repeat(32)
    a = np.empty((k // 512, 16))
    for p in range(k // 512):
        a[p, :8] = np.random.permutation(np.resize(levels, 8))
        for g in range(8):
            far = levels[np.abs(levels - a[p, g]) >= 10]
            a[p, g + 8] = far[np.random.randint(len(far))]
    return np.exp2(a.ravel()).repeat(32)


def f64(x):
    return np.asarray(x).astype(np.float64)


def striped(idx):
    return np.tile(idx.reshape(-1, 16).T, (8, 1)).astype(np.uint16)


def unstriped(offs):
    return offs[:16].T.reshape(-1).astype(np.int64)


E2M1 = np.array([0.0, 0.5, 1.0, 1.5, 2.0, 3.0, 4.0, 6.0, -0.0, -0.5, -1.0, -1.5, -2.0, -3.0, -4.0, -6.0])


def pack_weight(w, fmt):
    k, n = w.shape
    w = f64(np.asarray(w, np.float32).astype(ml_dtypes.bfloat16)).reshape(k // 32, 32, n)
    amax = np.abs(w).max(1)
    if fmt == "e4m3":
        byte = np.frexp(amax)[1] - 1 + 127 - 7
    else:
        mant, ex = np.frexp(amax / 6.0)
        byte = np.where(mant > 0.5, ex, ex - 1) + 127
    byte = np.clip(np.where(amax > 0, byte, 1), 1, 254)
    scaled = (w * np.exp2(127.0 - byte)[:, None, :]).reshape(k, n).astype(np.float32)
    by_word = np.ascontiguousarray(scaled.reshape(k // 512, 128, 4, n).transpose(0, 1, 3, 2))
    if fmt == "e4m3":
        words = by_word.astype(ml_dtypes.float8_e4m3fn).view(np.uint8)
    else:
        c = by_word.astype(ml_dtypes.float4_e2m1fn).view(np.uint8) & 0xF
        words = (c[..., 0::2] | (c[..., 1::2] << 4)).reshape(k // 512, 128, 2 * n)
    return np.ascontiguousarray(words), np.ascontiguousarray(byte.astype(np.uint8).reshape(k // 512, 16, n))


def unpack_weight(words, scales, fmt):
    g, _, n = scales.shape
    words = np.ascontiguousarray(words).reshape(g, 128, n, -1)
    if fmt == "e4m3":
        vals = words.view(ml_dtypes.float8_e4m3fn).astype(np.float64)
    else:
        nib = np.empty((g, 128, n, 4), np.uint8)
        nib[..., 0::2] = words & 0xF
        nib[..., 1::2] = words >> 4
        vals = E2M1[nib]
    vals = vals * np.repeat(np.exp2(scales.astype(np.float64) - 127.0), 8, axis=1)[..., None]
    return vals.transpose(0, 1, 3, 2).reshape(g * 512, n)


def silu(v):
    return v / (1.0 + np.exp(-np.maximum(v, -700.0)))


K, T, E, C, H, N = 512, 512, 4, 256, 512, 512


def by_expert(wq, xq):
    return np.concatenate([wq[e].T @ xq[:, e * C:(e + 1) * C] for e in range(E)], axis=1)


def setup_inputs():
    n = np.random.standard_normal
    s = mx_kscale(K)[:, None]
    u = mx_kscale(H)
    first = np.random.permutation(np.repeat(np.arange(E), T // E))
    second = (first + 1 + np.random.permutation(np.repeat(np.arange(E - 1), -(-T // (E - 1)))[:T])) % E
    while np.bincount(second, minlength=E).max() != T // E:
        load = np.bincount(second, minlength=E); hi, lo = int(load.argmax()), int(load.argmin())
        t = np.flatnonzero((second == hi) & (first != lo))[0]; second[t] = lo
    slot_token = np.empty(E * C, np.int64); pos = np.empty((2, T), np.int64); fill = np.zeros(E, np.int64)
    place = np.stack([np.random.permutation(C) for _ in range(E)])
    for r, deal in enumerate((first, second)):
        for t in np.random.permutation(T):
            e = deal[t]; j = e * C + place[e, fill[e]]; fill[e] += 1; slot_token[j] = t; pos[r, t] = j
    g = np.random.uniform(0.2, 0.8, T)
    w1 = [pack_weight(m, "e2m1") for m in n((E, K, H)) / np.sqrt(K) / s[None]]
    w3 = [pack_weight(m, "e2m1") for m in n((E, K, H)) / np.sqrt(K) / s[None] * u[None, None, :]]
    w2 = [pack_weight(m, "e2m1") for m in n((E, H, N)) / np.sqrt(H) / u[None, :, None]]
    return {
        "xT": (n((K, T)) * s).astype(np.float32),
        "w1_words": np.stack([m[0] for m in w1]),
        "w1_scales": np.stack([m[1] for m in w1]),
        "w3_words": np.stack([m[0] for m in w3]),
        "w3_scales": np.stack([m[1] for m in w3]),
        "w2_words": np.stack([m[0] for m in w2]),
        "w2_scales": np.stack([m[1] for m in w2]),
        "gate": np.stack([np.tile(g, (N, 1)), np.tile(1.0 - g, (N, 1))]).astype(np.float32),
        "offs": striped(slot_token),
        "pos1": striped(pos[0]),
        "pos2": striped(pos[1]),
    }


def reference(xT, w1_words, w1_scales, w3_words, w3_scales, w2_words, w2_scales, gate, offs, pos1, pos2):
    idx = unstriped(offs)
    w1 = np.stack([unpack_weight(w1_words[e], w1_scales[e], "e2m1") for e in range(E)])
    w3 = np.stack([unpack_weight(w3_words[e], w3_scales[e], "e2m1") for e in range(E)])
    w2 = np.stack([unpack_weight(w2_words[e], w2_scales[e], "e2m1") for e in range(E)])
    xq = mxq(f64(xT)[:, idx], 0, "e4m3")
    h = silu(by_expert(w1, xq))
    h = h * by_expert(w3, xq)
    y = by_expert(w2, mxq(h, 0, "e4m3"))
    return f64(gate[0]) * y[:, unstriped(pos1)] + f64(gate[1]) * y[:, unstriped(pos2)]

@@ -1,0 +1,249 @@
+from contextlib import ExitStack
+
+import concourse.mybir as mybir
+from concourse.masks import make_identity
+
+F32 = mybir.dt.float32
+BF16 = mybir.dt.bfloat16
+I32 = mybir.dt.int32
+U32 = mybir.dt.uint32
+U16 = mybir.dt.uint16
+U8 = mybir.dt.uint8
+FP8X4 = mybir.dt.float8_e4m3fn_x4
+FP4X4 = mybir.dt.float4_e2m1fn_x4
+ADD, MULT = mybir.AluOpType.add, mybir.AluOpType.mult
+SILU = mybir.ActivationFunctionType.Silu
+
+P = 128
+K, T, E, C, H, N = 512, 512, 4, 256, 512, 512
+S = E * C
+PACK = 4
+UNIT = 128
+UNITS = S // UNIT
+UNITS_PER_EXPERT = C // UNIT
+BLOCKS = N // P
+LIST_ROWS = 16
+PSUM_BANKS = 8
+
+HALF = T // 2
+X_ON_SCALAR = 96
+GATHER_CUTS = (0, 256, 640, 1024)
+ON_GPSIMD = (0,)
+TURNED_OUT_ON_VECTOR = (4,)
+LAST = E - 1
+RESULT_CUTS = ((0, 512, 768, 896, S),) + ((0, 512, S),) * (BLOCKS - 1)
+LAST_CUTS = (0, 384, T)
+
+FLOPS = 2 * S * (2 * K * H + H * N)
+
+
+def tile_moe_pln_glu_silu_kernel(
+    tc, xT, w1_words, w1_scales, w3_words, w3_scales, w2_words, w2_scales, gate, offs, pos1, pos2, out
+):
+    nc = tc.nc
+    with ExitStack() as ctx:
+        keep = ctx.enter_context(tc.tile_pool(name="keep", bufs=1))
+        work = ctx.enter_context(tc.tile_pool(name="work", bufs=8))
+        psum = ctx.enter_context(tc.psum_pool(name="psum", bufs=PSUM_BANKS))
+
+        def bank(shape):
+            return psum.tile(shape, F32, name="bank")
+
+        words = [keep.tile([P, E, 2 * H], U8, name=f"words{m}", align_bytes=64) for m in range(3)]
+        planes = [keep.tile([P, E, H], U8, name=f"planes{m}", align_bytes=64) for m in range(3)]
+
+        def zero_planes(m):
+            nc.vector.memset(planes[m][:].rearrange("p e i -> p (e i)").bitcast(I32), 0)
+
+        def load_words(m, dram, e0, e1):
+            nc.sync.dma_start(
+                words[m][:, e0:e1, :].bitcast(I32), dram.bitcast(I32)[e0:e1].rearrange("e o p i -> p (e o) i")
+            )
+
+        def load_scales(engines, m, dram):
+            rows = dram.bitcast(I32).rearrange("e o (Q r) i -> r Q (e o) i", r=4)
+            for r, engine in enumerate(engines):
+                engine.dma_start(planes[m][:].bitcast(I32)[r : P : 32], rows[r])
+
+        x_raw = [keep.tile([P, PACK, HALF], F32, name=f"x_raw{h}", align_bytes=64) for h in range(2)]
+        for h in range(2):
+            nc.sync.dma_start(x_raw[h][:], xT.rearrange("(p j) t -> p j t", j=PACK)[:, :, h * HALF : (h + 1) * HALF])
+        offs_sb = keep.tile([P, S // LIST_ROWS], U16, name="offs_sb")
+        nc.sync.dma_start(offs_sb[:], offs)
+
+        x_scales = keep.tile([P, T], U8, name="x_scales", align_bytes=64)
+        nc.gpsimd.memset(x_scales[:], 0)
+        warm = keep.tile([P, 1], F32, name="warm")
+        nc.vector.memset(warm[:], 0.0)
+        zero_planes(0)
+        zero_planes(1)
+        load_words(0, w1_words, 0, 1)
+        load_words(1, w3_words, 0, 1)
+        load_scales([nc.scalar, nc.scalar, nc.scalar, nc.sync], 0, w1_scales)
+        load_scales([nc.sync] * 4, 1, w3_scales)
+        nc.scalar.activation(warm[:], warm[:], SILU)
+        zero_planes(2)
+        ident = keep.tile([P, P], F32, name="ident")
+        make_identity(nc, ident[:])
+        load_words(0, w1_words, 1, E)
+        load_words(1, w3_words, 1, E)
+        load_scales([nc.sync] * 4, 2, w2_scales)
+        load_words(2, w2_words, 0, E)
+        pos_sb = [keep.tile([P, T // LIST_ROWS], U16, name=f"pos_sb{r}") for r in range(2)]
+        nc.sync.dma_start(pos_sb[0][:], pos1)
+        nc.sync.dma_start(pos_sb[1][:], pos2)
+        gates = [keep.tile([P, BLOCKS, T], F32, name=f"gates{r}") for r in range(2)]
+        for r in range(2):
+            nc.sync.dma_start(gates[r][:], gate[r].rearrange("(b p) t -> p b t", p=P))
+
+        x_codes = keep.tile([P, T], U32, name="x_codes", align_bytes=64)
+        for h in range(2):
+            x_bf = keep.tile([P, HALF, PACK], BF16, name=f"x_bf{h}", align_bytes=64)
+            source = x_raw[h][:].rearrange("p j t -> p t j")
+            nc.scalar.copy(x_bf[:, :X_ON_SCALAR, :], source[:, :X_ON_SCALAR, :])
+            nc.vector.tensor_copy(x_bf[:, X_ON_SCALAR:, :], source[:, X_ON_SCALAR:, :])
+            tokens = slice(h * HALF, (h + 1) * HALF)
+            nc.vector.quantize_mx(
+                out=x_codes[:, tokens].bitcast(FP8X4),
+                scales=x_scales[:, tokens],
+                in_=x_bf[:].rearrange("p t j -> p (t j)"),
+            )
+
+        slot_codes, slot_scales = {}, {}
+        for cut, (s0, s1) in enumerate(zip(GATHER_CUTS[:-1], GATHER_CUTS[1:])):
+            listed = offs_sb[:, s0 // LIST_ROWS : s1 // LIST_ROWS]
+            scales = keep.tile([P, s1 - s0], U8, name=f"slot_scales{cut}", align_bytes=64)
+            codes = keep.tile([P, s1 - s0], U32, name=f"slot_codes{cut}", align_bytes=64)
+            nc.vector.tensor_copy(scales[:], x_scales[:].indirect(listed))
+            nc.vector.tensor_copy(codes[:], x_codes[:].indirect(listed))
+            for s in range(s0, s1, UNIT):
+                slot_codes[s // UNIT] = codes[:, s - s0 : s - s0 + UNIT]
+                slot_scales[s // UNIT] = scales[:, s - s0 : s - s0 + UNIT]
+
+        h_codes = [keep.tile([P, C], U32, name=f"h_codes{e}", align_bytes=64) for e in range(E)]
+        h_scales = [keep.tile([P, C], U8, name=f"h_scales{e}", align_bytes=64) for e in range(E)]
+        a_banks, b_banks, act, up, hidden, turned, hidden_k = {}, {}, {}, {}, {}, {}, {}
+
+        def first_product(banks, m, unit):
+            e = unit // UNITS_PER_EXPERT
+            banks[unit] = bank([P, H])
+            nc.tensor.matmul_mx(
+                out=banks[unit][:],
+                lhsT=slot_codes[unit].bitcast(FP8X4),
+                lhsT_scale=slot_scales[unit],
+                rhs=words[m][:, e, :].bitcast(FP4X4),
+                rhs_scale=planes[m][:, e, :],
+                start=True,
+                stop=True,
+            )
+
+        def gate_product(unit):
+            first_product(a_banks, 0, unit)
+
+        def up_product(unit):
+            first_product(b_banks, 1, unit)
+
+        def activate(unit):
+            act[unit] = work.tile([P, H], F32, name="act")
+            nc.scalar.activation(act[unit][:], a_banks[unit][:], SILU)
+
+        def copy_up(unit):
+            if unit in ON_GPSIMD:
+                up[unit] = work.tile([P, H], F32, name="up")
+                nc.scalar.copy(up[unit][:], b_banks[unit][:])
+
+        def multiply(unit):
+            hidden[unit] = work.tile([P, H], BF16, name="hidden")
+            if unit in ON_GPSIMD:
+                nc.gpsimd.tensor_tensor(hidden[unit][:], act[unit][:], up[unit][:], MULT)
+            else:
+                nc.vector.tensor_tensor(hidden[unit][:], act[unit][:], b_banks[unit][:], MULT)
+
+        def turn(unit):
+            pairs = hidden[unit][:].bitcast(F32)
+            turned[unit] = bank([P, 2, UNIT])
+            for u in range(2):
+                nc.tensor.transpose(turned[unit][:, u, :], pairs[:, u : H // 2 : 2], ident[:])
+
+        def turn_out(unit):
+            e, place = unit // UNITS_PER_EXPERT, unit % UNITS_PER_EXPERT
+            if e == LAST or place == 0:
+                joined = 1 if e == LAST else UNITS_PER_EXPERT
+                hidden_k[unit] = work.tile([P, joined * UNIT * PACK], BF16, name="hidden_k", align_bytes=64)
+            else:
+                hidden_k[unit] = hidden_k[unit - place]
+            s0 = 0 if e == LAST else place * UNIT
+            copy = nc.vector.tensor_copy if unit in TURNED_OUT_ON_VECTOR else nc.scalar.copy
+            copy(
+                hidden_k[unit][:, s0 * PACK : (s0 + UNIT) * PACK].bitcast(F32).rearrange("p (s u) -> p s u", u=2),
+                turned[unit][:].rearrange("p u s -> p s u"),
+            )
+
+        def quantise(unit):
+            e, place = unit // UNITS_PER_EXPERT, unit % UNITS_PER_EXPERT
+            if e == LAST:
+                slots = slice(place * UNIT, (place + 1) * UNIT)
+            elif place == UNITS_PER_EXPERT - 1:
+                slots = slice(0, C)
+            else:
+                return
+            nc.vector.quantize_mx(
+                out=h_codes[e][:, slots].bitcast(FP8X4), scales=h_scales[e][:, slots], in_=hidden_k[unit][:]
+            )
+
+        stages = (
+            (gate_product, 0),
+            (up_product, 1),
+            (activate, 0),
+            (copy_up, 1),
+            (multiply, 1),
+            (turn, UNITS - 1),
+            (turn_out, UNITS - 1),
+            (quantise, UNITS),
+        )
+        for step in range(2 * UNITS):
+            for stage, lag in stages:
+                if 0 <= step - lag < UNITS:
+                    stage(step - lag)
+
+        y_sb = [keep.tile([P, S], F32, name=f"y_sb{b}") for b in range(BLOCKS)]
+        for b in range(BLOCKS):
+            for s0, s1 in zip(RESULT_CUTS[b][:-1], RESULT_CUTS[b][1:]):
+                y_bank = bank([P, s1 - s0])
+                for e in range(s0 // C, (s1 + C - 1) // C):
+                    m0, m1 = max(s0, e * C), min(s1, (e + 1) * C)
+                    nc.tensor.matmul_mx(
+                        out=y_bank[:, m0 - s0 : m1 - s0],
+                        lhsT=words[2][:, e, 2 * b * P : 2 * (b + 1) * P].bitcast(FP4X4),
+                        lhsT_scale=planes[2][:, e, b * P : (b + 1) * P],
+                        rhs=h_codes[e][:, m0 - e * C : m1 - e * C].bitcast(FP8X4),
+                        rhs_scale=h_scales[e][:, m0 - e * C : m1 - e * C],
+                        start=True,
+                        stop=True,
+                    )
+                copy = nc.vector.tensor_copy if b == 0 and s0 == 0 else nc.scalar.copy
+                copy(y_sb[b][:, s0:s1], y_bank[:])
+
+        parts = {(b, r): work.tile([P, T], F32, name=f"part{r}") for b in range(BLOCKS) for r in range(2)}
+
+        def pick(b, r, t0, t1):
+            listed = pos_sb[r][:, t0 // LIST_ROWS : t1 // LIST_ROWS]
+            nc.vector.tensor_tensor(
+                parts[b, r][:, t0:t1], y_sb[b][:].indirect(listed), gates[r][:, b, t0:t1], MULT
+            )
+
+        def add_and_store(b, t0, t1):
+            total = work.tile([P, t1 - t0], F32, name="total")
+            nc.vector.tensor_tensor(total[:], parts[b, 0][:, t0:t1], parts[b, 1][:, t0:t1], ADD)
+            nc.sync.dma_start(out[b * P : (b + 1) * P, t0:t1], total[:])
+
+        last = BLOCKS - 1
+        last_pieces = list(zip(LAST_CUTS[:-1], LAST_CUTS[1:]))
+        for b in range(BLOCKS):
+            pick(b, 0, 0, T)
+            if b > 0:
+                add_and_store(b - 1, 0, T)
+            for t0, t1 in last_pieces if b == last else [(0, T)]:
+                pick(b, 1, t0, t1)
+        for t0, t1 in last_pieces:
+            add_and_store(last, t0, t1)

@@ -32,6 +32,9 @@ ON_GPSIMD = (0,)
 TURNED_OUT_ON_VECTOR = (4,)
 LAST = E - 1
 RESULT_CUTS = ((0, 512, 768, 896, S),) + ((0, 512, S),) * (BLOCKS - 1)
+SUM_CUTS = ((0, T), (0, T), (0, T // 2, T))
+SUM_BANKS = (2, 3)
+BACK_BANKS = (4, 5, 6, 7)
 LAST_CUTS = (0, 384, T)
 
 FLOPS = 2 * S * (2 * K * H + H * N)
@@ -44,10 +47,12 @@ def tile_moe_pln_glu_silu_kernel(
     with ExitStack() as ctx:
         keep = ctx.enter_context(tc.tile_pool(name="keep", bufs=1))
         work = ctx.enter_context(tc.tile_pool(name="work", bufs=8))
-        psum = ctx.enter_context(tc.psum_pool(name="psum", bufs=PSUM_BANKS))
+        psum = ctx.enter_context(tc.psum_pool(name="psum", bufs=1))
+        taken = []
 
-        def bank(shape):
-            return psum.tile(shape, F32, name="bank")
+        def bank(shape, number=None):
+            taken.append(len(taken) % PSUM_BANKS if number is None else number)
+            return psum.tile(shape, F32, name=f"bank{taken[-1]}")
 
         words = [keep.tile([P, E, 2 * H], U8, name=f"words{m}", align_bytes=64) for m in range(3)]
         planes = [keep.tile([P, E, H], U8, name=f"planes{m}", align_bytes=64) for m in range(3)]
@@ -92,9 +97,8 @@ def tile_moe_pln_glu_silu_kernel(
         pos_sb = [keep.tile([P, T // LIST_ROWS], U16, name=f"pos_sb{r}") for r in range(2)]
         nc.sync.dma_start(pos_sb[0][:], pos1)
         nc.sync.dma_start(pos_sb[1][:], pos2)
-        gates = [keep.tile([P, BLOCKS, T], F32, name=f"gates{r}") for r in range(2)]
-        for r in range(2):
-            nc.sync.dma_start(gates[r][:], gate[r].rearrange("(b p) t -> p b t", p=P))
+        gates = keep.tile([P, 2, T], F32, name="gates")
+        nc.sync.dma_start(gates[:], gate[:, :P, :].rearrange("r p t -> p r t"))
 
         x_codes = keep.tile([P, T], U32, name="x_codes", align_bytes=64)
         for h in range(2):
@@ -143,27 +147,33 @@ def tile_moe_pln_glu_silu_kernel(
         def up_product(unit):
             first_product(b_banks, 1, unit)
 
+        def by_pair(sums):
+            return sums[:].rearrange("s (p u d) -> s u p d", u=2, d=2)
+
+        def paired(tile):
+            return tile[:].rearrange("s (u p d) -> s u p d", u=2, d=2)
+
         def activate(unit):
             act[unit] = work.tile([P, H], F32, name="act")
-            nc.scalar.activation(act[unit][:], a_banks[unit][:], SILU)
+            nc.scalar.activation(paired(act[unit]), by_pair(a_banks[unit]), SILU)
 
         def copy_up(unit):
             if unit in ON_GPSIMD:
                 up[unit] = work.tile([P, H], F32, name="up")
-                nc.scalar.copy(up[unit][:], b_banks[unit][:])
+                nc.scalar.copy(paired(up[unit]), by_pair(b_banks[unit]))
 
         def multiply(unit):
             hidden[unit] = work.tile([P, H], BF16, name="hidden")
             if unit in ON_GPSIMD:
                 nc.gpsimd.tensor_tensor(hidden[unit][:], act[unit][:], up[unit][:], MULT)
             else:
-                nc.vector.tensor_tensor(hidden[unit][:], act[unit][:], b_banks[unit][:], MULT)
+                nc.vector.tensor_tensor(paired(hidden[unit]), paired(act[unit]), by_pair(b_banks[unit]), MULT)
 
         def turn(unit):
             pairs = hidden[unit][:].bitcast(F32)
             turned[unit] = bank([P, 2, UNIT])
             for u in range(2):
-                nc.tensor.transpose(turned[unit][:, u, :], pairs[:, u : H // 2 : 2], ident[:])
+                nc.tensor.transpose(turned[unit][:, u, :], pairs[:, u * P : (u + 1) * P], ident[:])
 
         def turn_out(unit):
             e, place = unit // UNITS_PER_EXPERT, unit % UNITS_PER_EXPERT
@@ -229,7 +239,7 @@ def tile_moe_pln_glu_silu_kernel(
         def pick(b, r, t0, t1):
             listed = pos_sb[r][:, t0 // LIST_ROWS : t1 // LIST_ROWS]
             nc.vector.tensor_tensor(
-                parts[b, r][:, t0:t1], y_sb[b][:].indirect(listed), gates[r][:, b, t0:t1], MULT
+                parts[b, r][:, t0:t1], y_sb[b][:].indirect(listed), gates[:, r, t0:t1], MULT
             )
 
         def add_and_store(b, t0, t1):
@@ -237,13 +247,45 @@ def tile_moe_pln_glu_silu_kernel(
             nc.vector.tensor_tensor(total[:], parts[b, 0][:, t0:t1], parts[b, 1][:, t0:t1], ADD)
             nc.sync.dma_start(out[b * P : (b + 1) * P, t0:t1], total[:])
 
+        sums, stored = {}, []
+
+        def add_by_transposes(b, t0, t1):
+            count = (t1 - t0) // P
+            summed = bank([P, count, P], SUM_BANKS[len(sums) % 2])
+            for r in range(2):
+                for q in range(count):
+                    nc.tensor.matmul(
+                        summed[:, q, :], parts[b, r][:, t0 + q * P : t0 + (q + 1) * P], ident[:],
+                        start=r == 0 and q == 0, stop=r == 1 and q == count - 1, is_transpose=True,
+                    )
+            by_token = work.tile([P, count, P], F32, name="by_token")
+            nc.scalar.copy(by_token[:], summed[:])
+            sums[b, t0] = by_token
+
+        def turn_back_and_store(b, t0, t1):
+            by_token = sums[b, t0]
+            back = bank([P, t1 - t0], BACK_BANKS[len(stored)])
+            stored.append((b, t0))
+            for q in range((t1 - t0) // P):
+                nc.tensor.transpose(back[:, q * P : (q + 1) * P], by_token[:, q, :], ident[:])
+            total = work.tile([P, t1 - t0], F32, name="total")
+            nc.scalar.copy(total[:], back[:])
+            nc.sync.dma_start(out[b * P : (b + 1) * P, t0:t1], total[:])
+
         last = BLOCKS - 1
         last_pieces = list(zip(LAST_CUTS[:-1], LAST_CUTS[1:]))
-        for b in range(BLOCKS):
+        waiting = None
+        for b in range(last):
             pick(b, 0, 0, T)
-            if b > 0:
-                add_and_store(b - 1, 0, T)
-            for t0, t1 in last_pieces if b == last else [(0, T)]:
+            for t0, t1 in zip(SUM_CUTS[b][:-1], SUM_CUTS[b][1:]):
                 pick(b, 1, t0, t1)
+                add_by_transposes(b, t0, t1)
+                if waiting is not None:
+                    turn_back_and_store(*waiting)
+                waiting = (b, t0, t1)
+        turn_back_and_store(*waiting)
+        pick(last, 0, 0, T)
+        for t0, t1 in last_pieces:
+            pick(last, 1, t0, t1)
         for t0, t1 in last_pieces:
             add_and_store(last, t0, t1)

@@ -32,7 +32,7 @@ ON_GPSIMD = (0,)
 TURNED_OUT_ON_VECTOR = (4,)
 LAST = E - 1
 RESULT_CUTS = ((0, 512, 768, 896, S),) + ((0, 512, S),) * (BLOCKS - 1)
-SUM_CUTS = ((0, T), (0, T), (0, T // 2, T))
+SUMMED_ON_TENSOR = (T, T, T // 2)
 SUM_BANKS = (2, 3)
 BACK_BANKS = (4, 5, 6, 7)
 LAST_CUTS = (0, 384, T)
@@ -277,14 +277,14 @@ def tile_moe_pln_glu_silu_kernel(
         waiting = None
         for b in range(last):
             pick(b, 0, 0, T)
-            for t0, t1 in zip(SUM_CUTS[b][:-1], SUM_CUTS[b][1:]):
-                pick(b, 1, t0, t1)
-                add_by_transposes(b, t0, t1)
-                if waiting is not None:
-                    turn_back_and_store(*waiting)
-                waiting = (b, t0, t1)
+            pick(b, 1, 0, T)
+            add_by_transposes(b, 0, SUMMED_ON_TENSOR[b])
+            if waiting is not None:
+                turn_back_and_store(*waiting)
+            waiting = (b, 0, SUMMED_ON_TENSOR[b])
         turn_back_and_store(*waiting)
         pick(last, 0, 0, T)
+        add_and_store(last - 1, SUMMED_ON_TENSOR[last - 1], T)
         for t0, t1 in last_pieces:
             pick(last, 1, t0, t1)
         for t0, t1 in last_pieces:

@@ -28,8 +28,6 @@ PSUM_BANKS = 8
 HALF = T // 2
 X_ON_SCALAR = 96
 GATHER_CUTS = (0, 256, 640, 1024)
-ON_GPSIMD = (0,)
-TURNED_OUT_ON_VECTOR = (4,)
 LAST = E - 1
 RESULT_CUTS = ((0, 512, 768, 896, S),) + ((0, 512, S),) * (BLOCKS - 1)
 SUMMED_ON_TENSOR = (T, T, T // 2)
@@ -126,7 +124,7 @@ def tile_moe_pln_glu_silu_kernel(
 
         h_codes = [keep.tile([P, C], U32, name=f"h_codes{e}", align_bytes=64) for e in range(E)]
         h_scales = [keep.tile([P, C], U8, name=f"h_scales{e}", align_bytes=64) for e in range(E)]
-        a_banks, b_banks, act, up, hidden, turned, hidden_k = {}, {}, {}, {}, {}, {}, {}
+        a_banks, b_banks, act, hidden, turned, hidden_k = {}, {}, {}, {}, {}, {}
 
         def first_product(banks, m, unit):
             e = unit // UNITS_PER_EXPERT
@@ -157,17 +155,9 @@ def tile_moe_pln_glu_silu_kernel(
             act[unit] = work.tile([P, H], F32, name="act")
             nc.scalar.activation(paired(act[unit]), by_pair(a_banks[unit]), SILU)
 
-        def copy_up(unit):
-            if unit in ON_GPSIMD:
-                up[unit] = work.tile([P, H], F32, name="up")
-                nc.scalar.copy(paired(up[unit]), by_pair(b_banks[unit]))
-
         def multiply(unit):
             hidden[unit] = work.tile([P, H], BF16, name="hidden")
-            if unit in ON_GPSIMD:
-                nc.gpsimd.tensor_tensor(hidden[unit][:], act[unit][:], up[unit][:], MULT)
-            else:
-                nc.vector.tensor_tensor(paired(hidden[unit]), paired(act[unit]), by_pair(b_banks[unit]), MULT)
+            nc.vector.tensor_tensor(paired(hidden[unit]), paired(act[unit]), by_pair(b_banks[unit]), MULT)
 
         def turn(unit):
             pairs = hidden[unit][:].bitcast(F32)
@@ -183,8 +173,7 @@ def tile_moe_pln_glu_silu_kernel(
             else:
                 hidden_k[unit] = hidden_k[unit - place]
             s0 = 0 if e == LAST else place * UNIT
-            copy = nc.vector.tensor_copy if unit in TURNED_OUT_ON_VECTOR else nc.scalar.copy
-            copy(
+            nc.scalar.copy(
                 hidden_k[unit][:, s0 * PACK : (s0 + UNIT) * PACK].bitcast(F32).rearrange("p (s u) -> p s u", u=2),
                 turned[unit][:].rearrange("p u s -> p s u"),
             )
@@ -205,7 +194,6 @@ def tile_moe_pln_glu_silu_kernel(
             (gate_product, 0),
             (up_product, 1),
             (activate, 0),
-            (copy_up, 1),
             (multiply, 1),
             (turn, UNITS - 1),
             (turn_out, UNITS - 1),

@@ -81,8 +81,8 @@ def tile_moe_pln_glu_silu_kernel(
         zero_planes(0)
         zero_planes(1)
         load_words(0, w1_words, 0, 1)
+        load_scales([nc.sync] * 4, 0, w1_scales)
         load_words(1, w3_words, 0, 1)
-        load_scales([nc.scalar, nc.scalar, nc.scalar, nc.sync], 0, w1_scales)
         load_scales([nc.sync] * 4, 1, w3_scales)
         nc.scalar.activation(warm[:], warm[:], SILU)
         zero_planes(2)

@@ -23,17 +23,23 @@ UNITS = S // UNIT
 UNITS_PER_EXPERT = C // UNIT
 BLOCKS = N // P
 LIST_ROWS = 16
-PSUM_BANKS = 8
 
 HALF = T // 2
 X_ON_SCALAR = 96
 GATHER_CUTS = (0, 256, 640, 1024)
-LAST = E - 1
-RESULT_CUTS = ((0, 512, 768, 896, S),) + ((0, 512, S),) * (BLOCKS - 1)
+ON_GPSIMD = (0,)
+A_BANKS = (0, 1, 4, 5, 6, 2, 4, 5)
+B_BANKS = (2, 3, 7, 0, 1, 6, 2, 4)
+TURN_GROUPS = ((0, 1), (2, 3), (4, 5), (6,), (7,))
+TURN_BANKS = (3, 7, 1, 6, 0)
+TURN_LAG = 5
+RESULT_CUTS = ((0, 256, 512, 768, 896, S),) + ((0, 512, S),) * (BLOCKS - 1)
+RESULT_BANKS = ((5, 3, 7, 2, 4), (4, 1), (1, 4), (4, 1))
+RESULTS_ON_VECTOR = ((0, 2),)
 SUMMED_ON_TENSOR = (T, T, T // 2)
 SUM_BANKS = (2, 3)
-BACK_BANKS = (4, 5, 6, 7)
-LAST_CUTS = (0, 384, T)
+BACK_BANKS = (5, 6, 7)
+LAST_CUTS = (0, 256, 384, T)
 
 FLOPS = 2 * S * (2 * K * H + H * N)
 
@@ -46,11 +52,9 @@ def tile_moe_pln_glu_silu_kernel(
         keep = ctx.enter_context(tc.tile_pool(name="keep", bufs=1))
         work = ctx.enter_context(tc.tile_pool(name="work", bufs=8))
         psum = ctx.enter_context(tc.psum_pool(name="psum", bufs=1))
-        taken = []
 
-        def bank(shape, number=None):
-            taken.append(len(taken) % PSUM_BANKS if number is None else number)
-            return psum.tile(shape, F32, name=f"bank{taken[-1]}")
+        def bank(shape, number):
+            return psum.tile(shape, F32, name=f"bank{number}")
 
         words = [keep.tile([P, E, 2 * H], U8, name=f"words{m}", align_bytes=64) for m in range(3)]
         planes = [keep.tile([P, E, H], U8, name=f"planes{m}", align_bytes=64) for m in range(3)]
@@ -81,8 +85,8 @@ def tile_moe_pln_glu_silu_kernel(
         zero_planes(0)
         zero_planes(1)
         load_words(0, w1_words, 0, 1)
-        load_scales([nc.sync] * 4, 0, w1_scales)
         load_words(1, w3_words, 0, 1)
+        load_scales([nc.scalar, nc.scalar, nc.scalar, nc.sync], 0, w1_scales)
         load_scales([nc.sync] * 4, 1, w3_scales)
         nc.scalar.activation(warm[:], warm[:], SILU)
         zero_planes(2)
@@ -98,7 +102,7 @@ def tile_moe_pln_glu_silu_kernel(
         gates = keep.tile([P, 2, T], F32, name="gates")
         nc.sync.dma_start(gates[:], gate[:, :P, :].rearrange("r p t -> p r t"))
 
-        x_codes = keep.tile([P, T], U32, name="x_codes", align_bytes=64)
+        x_codes = keep.tile([P, T], U32, name="x_codes", tag="x_codes", align_bytes=64)
         for h in range(2):
             x_bf = keep.tile([P, HALF, PACK], BF16, name=f"x_bf{h}", align_bytes=64)
             source = x_raw[h][:].rearrange("p j t -> p t j")
@@ -124,11 +128,11 @@ def tile_moe_pln_glu_silu_kernel(
 
         h_codes = [keep.tile([P, C], U32, name=f"h_codes{e}", align_bytes=64) for e in range(E)]
         h_scales = [keep.tile([P, C], U8, name=f"h_scales{e}", align_bytes=64) for e in range(E)]
-        a_banks, b_banks, act, hidden, turned, hidden_k = {}, {}, {}, {}, {}, {}
+        a_banks, b_banks, act, hidden = {}, {}, {}, {}
 
-        def first_product(banks, m, unit):
+        def first_product(banks, numbers, m, unit):
             e = unit // UNITS_PER_EXPERT
-            banks[unit] = bank([P, H])
+            banks[unit] = bank([P, H], numbers[unit])
             nc.tensor.matmul_mx(
                 out=banks[unit][:],
                 lhsT=slot_codes[unit].bitcast(FP8X4),
@@ -139,12 +143,6 @@ def tile_moe_pln_glu_silu_kernel(
                 stop=True,
             )
 
-        def gate_product(unit):
-            first_product(a_banks, 0, unit)
-
-        def up_product(unit):
-            first_product(b_banks, 1, unit)
-
         def by_pair(sums):
             return sums[:].rearrange("s (p u d) -> s u p d", u=2, d=2)
 
@@ -152,62 +150,58 @@ def tile_moe_pln_glu_silu_kernel(
             return tile[:].rearrange("s (u p d) -> s u p d", u=2, d=2)
 
         def activate(unit):
+            first_product(a_banks, A_BANKS, 0, unit)
             act[unit] = work.tile([P, H], F32, name="act")
             nc.scalar.activation(paired(act[unit]), by_pair(a_banks[unit]), SILU)
 
         def multiply(unit):
-            hidden[unit] = work.tile([P, H], BF16, name="hidden")
-            nc.vector.tensor_tensor(paired(hidden[unit]), paired(act[unit]), by_pair(b_banks[unit]), MULT)
-
-        def turn(unit):
-            pairs = hidden[unit][:].bitcast(F32)
-            turned[unit] = bank([P, 2, UNIT])
-            for u in range(2):
-                nc.tensor.transpose(turned[unit][:, u, :], pairs[:, u * P : (u + 1) * P], ident[:])
-
-        def turn_out(unit):
-            e, place = unit // UNITS_PER_EXPERT, unit % UNITS_PER_EXPERT
-            if e == LAST or place == 0:
-                joined = 1 if e == LAST else UNITS_PER_EXPERT
-                hidden_k[unit] = work.tile([P, joined * UNIT * PACK], BF16, name="hidden_k", align_bytes=64)
+            first_product(b_banks, B_BANKS, 1, unit)
+            if unit in ON_GPSIMD:
+                up = work.tile([P, H], F32, name="up")
+                nc.scalar.copy(paired(up), by_pair(b_banks[unit]))
+                hidden[unit] = keep.tile([P, H], BF16, name="hidden_first", tag="x_codes", align_bytes=64)
+                nc.gpsimd.tensor_tensor(hidden[unit][:], act[unit][:], up[:], MULT)
             else:
-                hidden_k[unit] = hidden_k[unit - place]
-            s0 = 0 if e == LAST else place * UNIT
+                hidden[unit] = work.tile([P, H], BF16, name="hidden")
+                nc.vector.tensor_tensor(paired(hidden[unit]), paired(act[unit]), by_pair(b_banks[unit]), MULT)
+
+        turned_by_group = {}
+
+        def turn(group):
+            units, number = TURN_GROUPS[group], TURN_BANKS[group]
+            turned = bank([P, len(units), 2, UNIT], number)
+            for n, unit in reversed(list(enumerate(units))) if units[0] in ON_GPSIMD else enumerate(units):
+                pairs = hidden[unit][:].bitcast(F32)
+                for u in range(2):
+                    nc.tensor.transpose(turned[:, n, u, :], pairs[:, u * P : (u + 1) * P], ident[:])
+            turned_by_group[group] = turned
+
+        def quantise(group):
+            units, turned = TURN_GROUPS[group], turned_by_group[group]
+            hidden_k = work.tile([P, len(units) * UNIT * PACK], BF16, name="hidden_k", align_bytes=64)
             nc.scalar.copy(
-                hidden_k[unit][:, s0 * PACK : (s0 + UNIT) * PACK].bitcast(F32).rearrange("p (s u) -> p s u", u=2),
-                turned[unit][:].rearrange("p u s -> p s u"),
+                hidden_k[:].bitcast(F32).rearrange("p (n s u) -> p n s u", u=2, s=UNIT),
+                turned[:].rearrange("p n u s -> p n s u"),
             )
+            e, s0 = units[0] // UNITS_PER_EXPERT, units[0] % UNITS_PER_EXPERT * UNIT
+            slots = slice(s0, s0 + len(units) * UNIT)
+            nc.vector.quantize_mx(out=h_codes[e][:, slots].bitcast(FP8X4), scales=h_scales[e][:, slots], in_=hidden_k[:])
 
-        def quantise(unit):
-            e, place = unit // UNITS_PER_EXPERT, unit % UNITS_PER_EXPERT
-            if e == LAST:
-                slots = slice(place * UNIT, (place + 1) * UNIT)
-            elif place == UNITS_PER_EXPERT - 1:
-                slots = slice(0, C)
-            else:
-                return
-            nc.vector.quantize_mx(
-                out=h_codes[e][:, slots].bitcast(FP8X4), scales=h_scales[e][:, slots], in_=hidden_k[unit][:]
-            )
-
-        stages = (
-            (gate_product, 0),
-            (up_product, 1),
-            (activate, 0),
-            (multiply, 1),
-            (turn, UNITS - 1),
-            (turn_out, UNITS - 1),
-            (quantise, UNITS),
-        )
-        for step in range(2 * UNITS):
-            for stage, lag in stages:
-                if 0 <= step - lag < UNITS:
-                    stage(step - lag)
+        for s0, s1 in zip(GATHER_CUTS[:-1], GATHER_CUTS[1:]):
+            for stage in (activate, multiply):
+                for unit in range(s0 // UNIT, s1 // UNIT):
+                    stage(unit)
+                    if stage is multiply and unit >= TURN_LAG:
+                        turn(unit - TURN_LAG)
+        for group in range(UNITS - TURN_LAG, len(TURN_GROUPS)):
+            turn(group)
+        for group in range(len(TURN_GROUPS)):
+            quantise(group)
 
         y_sb = [keep.tile([P, S], F32, name=f"y_sb{b}") for b in range(BLOCKS)]
         for b in range(BLOCKS):
-            for s0, s1 in zip(RESULT_CUTS[b][:-1], RESULT_CUTS[b][1:]):
-                y_bank = bank([P, s1 - s0])
+            for piece, (s0, s1) in enumerate(zip(RESULT_CUTS[b][:-1], RESULT_CUTS[b][1:])):
+                y_bank = bank([P, s1 - s0], RESULT_BANKS[b][piece])
                 for e in range(s0 // C, (s1 + C - 1) // C):
                     m0, m1 = max(s0, e * C), min(s1, (e + 1) * C)
                     nc.tensor.matmul_mx(
@@ -219,7 +213,7 @@ def tile_moe_pln_glu_silu_kernel(
                         start=True,
                         stop=True,
                     )
-                copy = nc.vector.tensor_copy if b == 0 and s0 == 0 else nc.scalar.copy
+                copy = nc.vector.tensor_copy if (b, piece) in RESULTS_ON_VECTOR else nc.scalar.copy
                 copy(y_sb[b][:, s0:s1], y_bank[:])
 
         parts = {(b, r): work.tile([P, T], F32, name=f"part{r}") for b in range(BLOCKS) for r in range(2)}
@@ -272,8 +266,10 @@ def tile_moe_pln_glu_silu_kernel(
             waiting = (b, 0, SUMMED_ON_TENSOR[b])
         turn_back_and_store(*waiting)
         pick(last, 0, 0, T)
+        pick(last, 1, *last_pieces[0])
         add_and_store(last - 1, SUMMED_ON_TENSOR[last - 1], T)
-        for t0, t1 in last_pieces:
+        add_and_store(last, *last_pieces[0])
+        for t0, t1 in last_pieces[1:]:
             pick(last, 1, t0, t1)
-        for t0, t1 in last_pieces:
+        for t0, t1 in last_pieces[1:]:
             add_and_store(last, t0, t1)

@@ -26,19 +26,19 @@ LIST_ROWS = 16
 
 HALF = T // 2
 X_ON_SCALAR = 96
-GATHER_CUTS = (0, 256, 640, 1024)
-ON_GPSIMD = (0,)
-A_BANKS = (0, 1, 4, 5, 6, 2, 4, 5)
-B_BANKS = (2, 3, 7, 0, 1, 6, 2, 4)
-TURN_GROUPS = ((0, 1), (2, 3), (4, 5), (6,), (7,))
-TURN_BANKS = (3, 7, 1, 6, 0)
-TURN_LAG = 5
-RESULT_CUTS = ((0, 256, 512, 768, 896, S),) + ((0, 512, S),) * (BLOCKS - 1)
-RESULT_BANKS = ((5, 3, 7, 2, 4), (4, 1), (1, 4), (4, 1))
+GATHER_CUTS = (0, 128, 256, 512, 768, 1024)
+ON_GPSIMD = (0, 1)
+A_BANKS = (0, 1, 4, 5, 0, 1, 4, 5)
+B_BANKS = (2, 3, 6, 7, 2, 3, 0, 1)
+TURN_GROUPS = ((2, 3), (4, 5), (0, 1), (6,), (7,))
+TURN_BANKS = (6, 7, 4, 2, 3)
+FIRST_PIECES = tuple((units[0] * UNIT, (units[-1] + 1) * UNIT) for units in TURN_GROUPS)
+RESULT_PIECES = (FIRST_PIECES,) + (((0, 512), (512, S)),) * (BLOCKS - 1)
+RESULT_BANKS = ((5, 6, 7, 0, 1), (1, 4), (4, 1), (1, 4))
 RESULTS_ON_VECTOR = ((0, 2),)
 SUMMED_ON_TENSOR = (T, T, T // 2)
-SUM_BANKS = (2, 3)
-BACK_BANKS = (5, 6, 7)
+SUM_BANKS = (6, 7)
+BACK_BANKS = (2, 3, 5)
 LAST_CUTS = (0, 256, 384, T)
 
 FLOPS = 2 * S * (2 * K * H + H * N)
@@ -129,6 +129,7 @@ def tile_moe_pln_glu_silu_kernel(
         h_codes = [keep.tile([P, C], U32, name=f"h_codes{e}", align_bytes=64) for e in range(E)]
         h_scales = [keep.tile([P, C], U8, name=f"h_scales{e}", align_bytes=64) for e in range(E)]
         a_banks, b_banks, act, hidden = {}, {}, {}, {}
+        held = keep.tile([P, len(ON_GPSIMD), H], BF16, name="held", tag="x_codes", align_bytes=64)
 
         def first_product(banks, numbers, m, unit):
             e = unit // UNITS_PER_EXPERT
@@ -159,8 +160,8 @@ def tile_moe_pln_glu_silu_kernel(
             if unit in ON_GPSIMD:
                 up = work.tile([P, H], F32, name="up")
                 nc.scalar.copy(paired(up), by_pair(b_banks[unit]))
-                hidden[unit] = keep.tile([P, H], BF16, name="hidden_first", tag="x_codes", align_bytes=64)
-                nc.gpsimd.tensor_tensor(hidden[unit][:], act[unit][:], up[:], MULT)
+                hidden[unit] = held[:, ON_GPSIMD.index(unit), :]
+                nc.gpsimd.tensor_tensor(hidden[unit], act[unit][:], up[:], MULT)
             else:
                 hidden[unit] = work.tile([P, H], BF16, name="hidden")
                 nc.vector.tensor_tensor(paired(hidden[unit]), paired(act[unit]), by_pair(b_banks[unit]), MULT)
@@ -170,7 +171,7 @@ def tile_moe_pln_glu_silu_kernel(
         def turn(group):
             units, number = TURN_GROUPS[group], TURN_BANKS[group]
             turned = bank([P, len(units), 2, UNIT], number)
-            for n, unit in reversed(list(enumerate(units))) if units[0] in ON_GPSIMD else enumerate(units):
+            for n, unit in enumerate(units):
                 pairs = hidden[unit][:].bitcast(F32)
                 for u in range(2):
                     nc.tensor.transpose(turned[:, n, u, :], pairs[:, u * P : (u + 1) * P], ident[:])
@@ -187,20 +188,25 @@ def tile_moe_pln_glu_silu_kernel(
             slots = slice(s0, s0 + len(units) * UNIT)
             nc.vector.quantize_mx(out=h_codes[e][:, slots].bitcast(FP8X4), scales=h_scales[e][:, slots], in_=hidden_k[:])
 
-        for s0, s1 in zip(GATHER_CUTS[:-1], GATHER_CUTS[1:]):
-            for stage in (activate, multiply):
-                for unit in range(s0 // UNIT, s1 // UNIT):
-                    stage(unit)
-                    if stage is multiply and unit >= TURN_LAG:
-                        turn(unit - TURN_LAG)
-        for group in range(UNITS - TURN_LAG, len(TURN_GROUPS)):
+        def of_expert(stage, e):
+            for unit in range(e * UNITS_PER_EXPERT, (e + 1) * UNITS_PER_EXPERT):
+                stage(unit)
+
+        of_expert(activate, 0)
+        of_expert(multiply, 0)
+        of_expert(activate, 1)
+        for e in range(2, E):
+            of_expert(activate, e)
+            of_expert(multiply, e - 1)
+        of_expert(multiply, E - 1)
+        for group in range(len(TURN_GROUPS)):
             turn(group)
         for group in range(len(TURN_GROUPS)):
             quantise(group)
 
         y_sb = [keep.tile([P, S], F32, name=f"y_sb{b}") for b in range(BLOCKS)]
         for b in range(BLOCKS):
-            for piece, (s0, s1) in enumerate(zip(RESULT_CUTS[b][:-1], RESULT_CUTS[b][1:])):
+            for piece, (s0, s1) in enumerate(RESULT_PIECES[b]):
                 y_bank = bank([P, s1 - s0], RESULT_BANKS[b][piece])
                 for e in range(s0 // C, (s1 + C - 1) // C):
                     m0, m1 = max(s0, e * C), min(s1, (e + 1) * C)

@@ -24,21 +24,22 @@ UNITS_PER_EXPERT = C // UNIT
 BLOCKS = N // P
 LIST_ROWS = 16
 
-HALF = T // 2
-X_ON_SCALAR = 96
-GATHER_CUTS = (0, 128, 256, 512, 768, 1024)
+X_CUTS = (0, 256, 384, T)
+SCALAR_EIGHTHS = 3
+GATHER_CUTS = (0, 128, 256, 640, 1024)
+UNIT_RUNS = ((0, 1), (2, 3, 4), (5, 6, 7))
 ON_GPSIMD = (0, 1)
-A_BANKS = (0, 1, 4, 5, 0, 1, 4, 5)
-B_BANKS = (2, 3, 6, 7, 2, 3, 0, 1)
+A_BANKS = (0, 1, 4, 5, 0, 4, 5, 0)
+B_BANKS = (2, 3, 6, 7, 1, 2, 3, 4)
 TURN_GROUPS = ((2, 3), (4, 5), (0, 1), (6,), (7,))
-TURN_BANKS = (6, 7, 4, 2, 3)
+TURN_BANKS = (6, 7, 5, 1, 2)
 FIRST_PIECES = tuple((units[0] * UNIT, (units[-1] + 1) * UNIT) for units in TURN_GROUPS)
 RESULT_PIECES = (FIRST_PIECES,) + (((0, 512), (512, S)),) * (BLOCKS - 1)
-RESULT_BANKS = ((5, 6, 7, 0, 1), (1, 4), (4, 1), (1, 4))
+RESULT_BANKS = ((0, 6, 7, 3, 4), (4, 5), (5, 4), (4, 5))
 RESULTS_ON_VECTOR = ((0, 2),)
 SUMMED_ON_TENSOR = (T, T, T // 2)
 SUM_BANKS = (6, 7)
-BACK_BANKS = (2, 3, 5)
+BACK_BANKS = (1, 2, 0)
 LAST_CUTS = (0, 256, 384, T)
 
 FLOPS = 2 * S * (2 * K * H + H * N)
@@ -50,6 +51,7 @@ def tile_moe_pln_glu_silu_kernel(
     nc = tc.nc
     with ExitStack() as ctx:
         keep = ctx.enter_context(tc.tile_pool(name="keep", bufs=1))
+        rounding = ctx.enter_context(tc.tile_pool(name="rounding", bufs=2))
         work = ctx.enter_context(tc.tile_pool(name="work", bufs=8))
         psum = ctx.enter_context(tc.psum_pool(name="psum", bufs=1))
 
@@ -72,9 +74,10 @@ def tile_moe_pln_glu_silu_kernel(
             for r, engine in enumerate(engines):
                 engine.dma_start(planes[m][:].bitcast(I32)[r : P : 32], rows[r])
 
-        x_raw = [keep.tile([P, PACK, HALF], F32, name=f"x_raw{h}", align_bytes=64) for h in range(2)]
-        for h in range(2):
-            nc.sync.dma_start(x_raw[h][:], xT.rearrange("(p j) t -> p j t", j=PACK)[:, :, h * HALF : (h + 1) * HALF])
+        pieces = list(zip(X_CUTS[:-1], X_CUTS[1:]))
+        x_raw = [keep.tile([P, PACK, t1 - t0], F32, name=f"x_raw{t0}", align_bytes=64) for t0, t1 in pieces]
+        for raw, (t0, t1) in zip(x_raw, pieces):
+            nc.sync.dma_start(raw[:], xT.rearrange("(p j) t -> p j t", j=PACK)[:, :, t0:t1])
         offs_sb = keep.tile([P, S // LIST_ROWS], U16, name="offs_sb")
         nc.sync.dma_start(offs_sb[:], offs)
 
@@ -103,12 +106,13 @@ def tile_moe_pln_glu_silu_kernel(
         nc.sync.dma_start(gates[:], gate[:, :P, :].rearrange("r p t -> p r t"))
 
         x_codes = keep.tile([P, T], U32, name="x_codes", tag="x_codes", align_bytes=64)
-        for h in range(2):
-            x_bf = keep.tile([P, HALF, PACK], BF16, name=f"x_bf{h}", align_bytes=64)
-            source = x_raw[h][:].rearrange("p j t -> p t j")
-            nc.scalar.copy(x_bf[:, :X_ON_SCALAR, :], source[:, :X_ON_SCALAR, :])
-            nc.vector.tensor_copy(x_bf[:, X_ON_SCALAR:, :], source[:, X_ON_SCALAR:, :])
-            tokens = slice(h * HALF, (h + 1) * HALF)
+        for raw, (t0, t1) in zip(x_raw, pieces):
+            x_bf = rounding.tile([P, t1 - t0, PACK], BF16, name="x_bf", align_bytes=64)
+            source = raw[:].rearrange("p j t -> p t j")
+            share = (t1 - t0) * SCALAR_EIGHTHS // 8
+            nc.scalar.copy(x_bf[:, :share, :], source[:, :share, :])
+            nc.vector.tensor_copy(x_bf[:, share:, :], source[:, share:, :])
+            tokens = slice(t0, t1)
             nc.vector.quantize_mx(
                 out=x_codes[:, tokens].bitcast(FP8X4),
                 scales=x_scales[:, tokens],
@@ -188,17 +192,10 @@ def tile_moe_pln_glu_silu_kernel(
             slots = slice(s0, s0 + len(units) * UNIT)
             nc.vector.quantize_mx(out=h_codes[e][:, slots].bitcast(FP8X4), scales=h_scales[e][:, slots], in_=hidden_k[:])
 
-        def of_expert(stage, e):
-            for unit in range(e * UNITS_PER_EXPERT, (e + 1) * UNITS_PER_EXPERT):
-                stage(unit)
-
-        of_expert(activate, 0)
-        of_expert(multiply, 0)
-        of_expert(activate, 1)
-        for e in range(2, E):
-            of_expert(activate, e)
-            of_expert(multiply, e - 1)
-        of_expert(multiply, E - 1)
+        for run in UNIT_RUNS:
+            for stage in (activate, multiply):
+                for unit in run:
+                    stage(unit)
         for group in range(len(TURN_GROUPS)):
             turn(group)
         for group in range(len(TURN_GROUPS)):

@@ -82,19 +82,20 @@ def tile_moe_pln_glu_silu_kernel(
         nc.sync.dma_start(offs_sb[:], offs)
 
         x_scales = keep.tile([P, T], U8, name="x_scales", align_bytes=64)
-        nc.gpsimd.memset(x_scales[:], 0)
         warm = keep.tile([P, 1], F32, name="warm")
         nc.vector.memset(warm[:], 0.0)
         zero_planes(0)
         zero_planes(1)
+        nc.vector.memset(x_scales[:].bitcast(I32), 0)
         load_words(0, w1_words, 0, 1)
+        load_scales([nc.sync] * 4, 0, w1_scales)
         load_words(1, w3_words, 0, 1)
-        load_scales([nc.scalar, nc.scalar, nc.scalar, nc.sync], 0, w1_scales)
         load_scales([nc.sync] * 4, 1, w3_scales)
         nc.scalar.activation(warm[:], warm[:], SILU)
         zero_planes(2)
         ident = keep.tile([P, P], F32, name="ident")
-        make_identity(nc, ident[:])
+        nc.vector.memset(ident[:], 0.0)
+        make_identity(nc, ident[:], nomemset=True)
         load_words(0, w1_words, 1, E)
         load_words(1, w3_words, 1, E)
         load_scales([nc.sync] * 4, 2, w2_scales)

@@ -24,7 +24,7 @@ UNITS_PER_EXPERT = C // UNIT
 BLOCKS = N // P
 LIST_ROWS = 16
 
-X_CUTS = (0, 256, 384, T)
+X_CUTS = (0, 256, T)
 SCALAR_EIGHTHS = 3
 GATHER_CUTS = (0, 128, 256, 640, 1024)
 UNIT_RUNS = ((0, 1), (2, 3, 4), (5, 6, 7))
@@ -96,7 +96,8 @@ def tile_moe_pln_glu_silu_kernel(
         ident = keep.tile([P, P], F32, name="ident")
         nc.vector.memset(ident[:], 0.0)
         make_identity(nc, ident[:], nomemset=True)
-        load_words(0, w1_words, 1, E)
+        load_words(0, w1_words, 1, 2)
+        load_words(0, w1_words, 2, E)
         load_words(1, w3_words, 1, E)
         load_scales([nc.sync] * 4, 2, w2_scales)
         load_words(2, w2_words, 0, E)

@@ -13,6 +13,7 @@ FP8X4 = mybir.dt.float8_e4m3fn_x4
 FP4X4 = mybir.dt.float4_e2m1fn_x4
 ADD, MULT = mybir.AluOpType.add, mybir.AluOpType.mult
 SILU = mybir.ActivationFunctionType.Silu
+COPY = mybir.ActivationFunctionType.Copy
 
 P = 128
 K, T, E, C, H, N = 512, 512, 4, 256, 512, 512
@@ -37,9 +38,7 @@ FIRST_PIECES = tuple((units[0] * UNIT, (units[-1] + 1) * UNIT) for units in TURN
 RESULT_PIECES = (FIRST_PIECES,) + (((0, 512), (512, S)),) * (BLOCKS - 1)
 RESULT_BANKS = ((0, 6, 7, 3, 4), (4, 5), (5, 4), (4, 5))
 RESULTS_ON_VECTOR = ((0, 2),)
-SUMMED_ON_TENSOR = (T, T, T // 2)
-SUM_BANKS = (6, 7)
-BACK_BANKS = (1, 2, 0)
+HALVES = (0, 256, T)
 LAST_CUTS = (0, 256, 384, T)
 
 FLOPS = 2 * S * (2 * K * H + H * N)
@@ -204,7 +203,8 @@ def tile_moe_pln_glu_silu_kernel(
             quantise(group)
 
         y_sb = [keep.tile([P, S], F32, name=f"y_sb{b}") for b in range(BLOCKS)]
-        for b in range(BLOCKS):
+
+        def results(b):
             for piece, (s0, s1) in enumerate(RESULT_PIECES[b]):
                 y_bank = bank([P, s1 - s0], RESULT_BANKS[b][piece])
                 for e in range(s0 // C, (s1 + C - 1) // C):
@@ -221,60 +221,23 @@ def tile_moe_pln_glu_silu_kernel(
                 copy = nc.vector.tensor_copy if (b, piece) in RESULTS_ON_VECTOR else nc.scalar.copy
                 copy(y_sb[b][:, s0:s1], y_bank[:])
 
-        parts = {(b, r): work.tile([P, T], F32, name=f"part{r}") for b in range(BLOCKS) for r in range(2)}
-
-        def pick(b, r, t0, t1):
-            listed = pos_sb[r][:, t0 // LIST_ROWS : t1 // LIST_ROWS]
-            nc.vector.tensor_tensor(
-                parts[b, r][:, t0:t1], y_sb[b][:].indirect(listed), gates[:, r, t0:t1], MULT
-            )
-
-        def add_and_store(b, t0, t1):
-            total = work.tile([P, t1 - t0], F32, name="total")
-            nc.vector.tensor_tensor(total[:], parts[b, 0][:, t0:t1], parts[b, 1][:, t0:t1], ADD)
-            nc.sync.dma_start(out[b * P : (b + 1) * P, t0:t1], total[:])
-
-        sums, stored = {}, []
-
-        def add_by_transposes(b, t0, t1):
-            count = (t1 - t0) // P
-            summed = bank([P, count, P], SUM_BANKS[len(sums) % 2])
-            for r in range(2):
-                for q in range(count):
-                    nc.tensor.matmul(
-                        summed[:, q, :], parts[b, r][:, t0 + q * P : t0 + (q + 1) * P], ident[:],
-                        start=r == 0 and q == 0, stop=r == 1 and q == count - 1, is_transpose=True,
-                    )
-            by_token = work.tile([P, count, P], F32, name="by_token")
-            nc.scalar.copy(by_token[:], summed[:])
-            sums[b, t0] = by_token
-
-        def turn_back_and_store(b, t0, t1):
-            by_token = sums[b, t0]
-            back = bank([P, t1 - t0], BACK_BANKS[len(stored)])
-            stored.append((b, t0))
-            for q in range((t1 - t0) // P):
-                nc.tensor.transpose(back[:, q * P : (q + 1) * P], by_token[:, q, :], ident[:])
-            total = work.tile([P, t1 - t0], F32, name="total")
-            nc.scalar.copy(total[:], back[:])
-            nc.sync.dma_start(out[b * P : (b + 1) * P, t0:t1], total[:])
-
-        last = BLOCKS - 1
-        last_pieces = list(zip(LAST_CUTS[:-1], LAST_CUTS[1:]))
-        waiting = None
-        for b in range(last):
-            pick(b, 0, 0, T)
-            pick(b, 1, 0, T)
-            add_by_transposes(b, 0, SUMMED_ON_TENSOR[b])
-            if waiting is not None:
-                turn_back_and_store(*waiting)
-            waiting = (b, 0, SUMMED_ON_TENSOR[b])
-        turn_back_and_store(*waiting)
-        pick(last, 0, 0, T)
-        pick(last, 1, *last_pieces[0])
-        add_and_store(last - 1, SUMMED_ON_TENSOR[last - 1], T)
-        add_and_store(last, *last_pieces[0])
-        for t0, t1 in last_pieces[1:]:
-            pick(last, 1, t0, t1)
-        for t0, t1 in last_pieces[1:]:
-            add_and_store(last, t0, t1)
+        results(0)
+        for b in range(BLOCKS):
+            cuts = LAST_CUTS if b == BLOCKS - 1 else HALVES
+            spans = [slice(t0, t1) for t0, t1 in zip(cuts[:-1], cuts[1:])]
+            first = work.tile([P, T], F32, name="first")
+            second = work.tile([P, T], F32, name="second")
+            gated = work.tile([P, T], F32, name="gated")
+            total = work.tile([P, T], F32, name="total")
+            nc.vector.tensor_tensor(first[:], y_sb[b][:].indirect(pos_sb[0][:]), gates[:, 0, :], MULT)
+            nc.scalar.activation(second[:], y_sb[b][:].indirect(pos_sb[1][:]), COPY)
+            if b + 1 < BLOCKS:
+                results(b + 1)
+            for span in spans:
+                nc.vector.tensor_tensor(gated[:, span], second[:, span], gates[:, 1, span], MULT)
+            for span in spans:
+                nc.vector.tensor_tensor(total[:, span], first[:, span], gated[:, span], ADD)
+                if b == BLOCKS - 1:
+                    nc.sync.dma_start(out[b * P : (b + 1) * P, span], total[:, span])
+            if b < BLOCKS - 1:
+                nc.sync.dma_start(out[b * P : (b + 1) * P, :], total[:])

@@ -35,10 +35,11 @@ B_BANKS = (2, 3, 6, 7, 1, 2, 3, 4)
 TURN_GROUPS = ((2, 3), (4, 5), (0, 1), (6,), (7,))
 TURN_BANKS = (6, 7, 5, 1, 2)
 FIRST_PIECES = tuple((units[0] * UNIT, (units[-1] + 1) * UNIT) for units in TURN_GROUPS)
-RESULT_PIECES = (FIRST_PIECES,) + (((0, 512), (512, S)),) * (BLOCKS - 1)
-RESULT_BANKS = ((0, 6, 7, 3, 4), (4, 5), (5, 4), (4, 5))
-RESULTS_ON_VECTOR = ((0, 2),)
-HALVES = (0, 256, T)
+FIRST_BANKS = (0, 6, 7, 3, 4)
+FIRST_ON_VECTOR = (2,)
+EXPERT_PAIRS = ((1, 2), (0, 3))
+LATER_BANKS = {1: (5, 1), 2: (3, 4), 3: (5, 1)}
+GATE_BANKS = (7, 6)
 LAST_CUTS = (0, 256, 384, T)
 
 FLOPS = 2 * S * (2 * K * H + H * N)
@@ -57,7 +58,7 @@ def tile_moe_pln_glu_silu_kernel(
         def bank(shape, number):
             return psum.tile(shape, F32, name=f"bank{number}")
 
-        words = [keep.tile([P, E, 2 * H], U8, name=f"words{m}", align_bytes=64) for m in range(3)]
+        words = [keep.tile([P, E, 2 * H], U8, name=f"words{m}", align_bytes=64) for m in range(2)]
         planes = [keep.tile([P, E, H], U8, name=f"planes{m}", align_bytes=64) for m in range(3)]
 
         def zero_planes(m):
@@ -99,12 +100,20 @@ def tile_moe_pln_glu_silu_kernel(
         load_words(0, w1_words, 2, E)
         load_words(1, w3_words, 1, E)
         load_scales([nc.sync] * 4, 2, w2_scales)
-        load_words(2, w2_words, 0, E)
+        w2_rows = w2_words.bitcast(I32).rearrange("e o p i -> p (e o) i")
+        first_w2 = keep.tile([P, E, 2 * P], U8, name="first_w2", tag="first_w2", align_bytes=64)
+        later_w2 = keep.tile([P, E, 2 * (N - P)], U8, name="later_w2", align_bytes=64)
+        nc.sync.dma_start(first_w2[:].bitcast(I32), w2_rows[:, :, : P // 2])
+        nc.sync.dma_start(later_w2[:].bitcast(I32), w2_rows[:, :, P // 2 :])
         pos_sb = [keep.tile([P, T // LIST_ROWS], U16, name=f"pos_sb{r}") for r in range(2)]
         nc.sync.dma_start(pos_sb[0][:], pos1)
         nc.sync.dma_start(pos_sb[1][:], pos2)
-        gates = keep.tile([P, 2, T], F32, name="gates")
-        nc.sync.dma_start(gates[:], gate[:, :P, :].rearrange("r p t -> p r t"))
+        first_gate = keep.tile([P, T], F32, name="first_gate")
+        nc.sync.dma_start(first_gate[:], gate[0, :P, :])
+        gate_columns = [keep.tile([P, T // P], F32, name=f"gate_columns{r}") for r in range(2)]
+        with nc.allow_non_contiguous_dma(reason="one gate value a partition"):
+            for r in (1, 0):
+                nc.sync.dma_start(gate_columns[r][:], gate[r, 0, :].rearrange("(q p) -> p q", p=P))
 
         x_codes = keep.tile([P, T], U32, name="x_codes", tag="x_codes", align_bytes=64)
         for raw, (t0, t1) in zip(x_raw, pieces):
@@ -202,42 +211,97 @@ def tile_moe_pln_glu_silu_kernel(
         for group in range(len(TURN_GROUPS)):
             quantise(group)
 
-        y_sb = [keep.tile([P, S], F32, name=f"y_sb{b}") for b in range(BLOCKS)]
+        y_sb = {}
 
-        def results(b):
-            for piece, (s0, s1) in enumerate(RESULT_PIECES[b]):
-                y_bank = bank([P, s1 - s0], RESULT_BANKS[b][piece])
-                for e in range(s0 // C, (s1 + C - 1) // C):
-                    m0, m1 = max(s0, e * C), min(s1, (e + 1) * C)
-                    nc.tensor.matmul_mx(
-                        out=y_bank[:, m0 - s0 : m1 - s0],
-                        lhsT=words[2][:, e, 2 * b * P : 2 * (b + 1) * P].bitcast(FP4X4),
-                        lhsT_scale=planes[2][:, e, b * P : (b + 1) * P],
-                        rhs=h_codes[e][:, m0 - e * C : m1 - e * C].bitcast(FP8X4),
-                        rhs_scale=h_scales[e][:, m0 - e * C : m1 - e * C],
-                        start=True,
-                        stop=True,
-                    )
-                copy = nc.vector.tensor_copy if (b, piece) in RESULTS_ON_VECTOR else nc.scalar.copy
-                copy(y_sb[b][:, s0:s1], y_bank[:])
+        def second_product(target, b, e, c0, c1):
+            weights = first_w2[:, e, :] if b == 0 else later_w2[:, e, 2 * (b - 1) * P : 2 * b * P]
+            nc.tensor.matmul_mx(
+                out=target,
+                lhsT=weights.bitcast(FP4X4),
+                lhsT_scale=planes[2][:, e, b * P : (b + 1) * P],
+                rhs=h_codes[e][:, c0:c1].bitcast(FP8X4),
+                rhs_scale=h_scales[e][:, c0:c1],
+                start=True,
+                stop=True,
+            )
 
-        results(0)
-        for b in range(BLOCKS):
-            cuts = LAST_CUTS if b == BLOCKS - 1 else HALVES
-            spans = [slice(t0, t1) for t0, t1 in zip(cuts[:-1], cuts[1:])]
-            first = work.tile([P, T], F32, name="first")
-            second = work.tile([P, T], F32, name="second")
-            gated = work.tile([P, T], F32, name="gated")
-            total = work.tile([P, T], F32, name="total")
-            nc.vector.tensor_tensor(first[:], y_sb[b][:].indirect(pos_sb[0][:]), gates[:, 0, :], MULT)
-            nc.scalar.activation(second[:], y_sb[b][:].indirect(pos_sb[1][:]), COPY)
-            if b + 1 < BLOCKS:
-                results(b + 1)
-            for span in spans:
-                nc.vector.tensor_tensor(gated[:, span], second[:, span], gates[:, 1, span], MULT)
-            for span in spans:
-                nc.vector.tensor_tensor(total[:, span], first[:, span], gated[:, span], ADD)
-                if b == BLOCKS - 1:
-                    nc.sync.dma_start(out[b * P : (b + 1) * P, span], total[:, span])
-            if b < BLOCKS - 1:
-                nc.sync.dma_start(out[b * P : (b + 1) * P, :], total[:])
+        def first_results():
+            y_sb[0] = keep.tile([P, S], F32, name="y_sb0", align_bytes=64)
+            for piece, (s0, s1) in enumerate(FIRST_PIECES):
+                y_bank = bank([P, s1 - s0], FIRST_BANKS[piece])
+                e = s0 // C
+                second_product(y_bank[:], 0, e, s0 - e * C, s1 - e * C)
+                copy = nc.vector.tensor_copy if piece in FIRST_ON_VECTOR else nc.scalar.copy
+                copy(y_sb[0][:, s0:s1], y_bank[:])
+
+        def later_results(b, pair, copy):
+            if pair == 0:
+                tag = ("y_sb0", "first_w2", "y_sb2", "y_sb0")[b]
+                y_sb[b] = keep.tile([P, S], F32, name=f"y_sb{b}", tag=tag, align_bytes=64)
+            e0, e1 = EXPERT_PAIRS[pair]
+            y_bank = bank([P, 2, C], LATER_BANKS[b][pair])
+            for n, e in enumerate((e0, e1)):
+                second_product(y_bank[:, n, :], b, e, 0, C)
+            copy(y_sb[b][:].rearrange("p (e c) -> p e c", c=C)[:, e0 : e1 + 1 : e1 - e0, :], y_bank[:])
+
+        parts = {(b, r): work.tile([P, T], F32, name="part") for b in range(BLOCKS) for r in range(2)}
+        picked = {}
+        gate_rows = {}
+
+        def spread_gate(r):
+            gate_rows[r] = bank([P, T], GATE_BANKS[r])
+            for q in range(T // P):
+                nc.tensor.transpose(
+                    gate_rows[r][:, q * P : (q + 1) * P], gate_columns[r][:, q : q + 1].to_broadcast([P, P]), ident[:]
+                )
+
+        def listed(r, t0, t1):
+            return pos_sb[r][:, t0 // LIST_ROWS : t1 // LIST_ROWS]
+
+        def pick_gated(b):
+            nc.vector.tensor_tensor(parts[b, 0][:], y_sb[b][:].indirect(listed(0, 0, T)), first_gate[:], MULT)
+
+        def pick(b, r, t0, t1):
+            if b == 0:
+                picked[b, r] = keep.tile([P, T], F32, name="picked0", tag=f"h_codes{E - 1}", align_bytes=64)
+            elif t0 == 0:
+                picked[b, r] = work.tile([P, T], F32, name="picked")
+            nc.scalar.activation(picked[b, r][:, t0:t1], y_sb[b][:].indirect(listed(r, t0, t1)), COPY)
+
+        def weigh(b, r, t0, t1):
+            nc.vector.tensor_tensor(parts[b, r][:, t0:t1], picked[b, r][:, t0:t1], gate_rows[r][:, t0:t1], MULT)
+
+        def add_and_store(engine, b, t0, t1):
+            total = work.tile([P, t1 - t0], F32, name="total")
+            engine.tensor_tensor(total[:], parts[b, 0][:, t0:t1], parts[b, 1][:, t0:t1], ADD)
+            nc.sync.dma_start(out[b * P : (b + 1) * P, t0:t1], total[:])
+
+        first_results()
+        pick_gated(0)
+        for b in (1, 2):
+            later_results(b, 0, nc.scalar.copy)
+            later_results(b, 1, nc.scalar.copy)
+            pick_gated(b)
+        spread_gate(1)
+        for b in (0, 1, 2):
+            pick(b, 1, 0, T)
+            weigh(b, 1, 0, T)
+            if b < 2:
+                add_and_store(nc.gpsimd, b, 0, T)
+                later_results(3, b, nc.vector.tensor_copy)
+        spread_gate(0)
+        t0, t1, t2, t3 = LAST_CUTS
+        pick(3, 0, t0, t1)
+        pick(3, 1, t0, t1)
+        pick(3, 0, t1, t3)
+        pick(3, 1, t1, t2)
+        pick(3, 1, t2, t3)
+        weigh(3, 0, t0, t1)
+        add_and_store(nc.vector, 2, 0, T)
+        weigh(3, 1, t0, t1)
+        weigh(3, 0, t1, t3)
+        add_and_store(nc.vector, 3, t0, t1)
+        weigh(3, 1, t1, t2)
+        weigh(3, 1, t2, t3)
+        add_and_store(nc.vector, 3, t1, t2)
+        add_and_store(nc.vector, 3, t2, t3)

@@ -39,7 +39,8 @@ FIRST_BANKS = (0, 6, 7, 3, 4)
 FIRST_ON_VECTOR = (2,)
 EXPERT_PAIRS = ((1, 2), (0, 3))
 LATER_BANKS = {1: (5, 1), 2: (3, 4), 3: (5, 1)}
-GATE_BANKS = (7, 6)
+GATE_BANKS = (4, 3)
+W2_TILES = ((0, 1), (1, 3), (3, 4))
 LAST_CUTS = (0, 256, 384, T)
 
 FLOPS = 2 * S * (2 * K * H + H * N)
@@ -101,10 +102,12 @@ def tile_moe_pln_glu_silu_kernel(
         load_words(1, w3_words, 1, E)
         load_scales([nc.sync] * 4, 2, w2_scales)
         w2_rows = w2_words.bitcast(I32).rearrange("e o p i -> p (e o) i")
-        first_w2 = keep.tile([P, E, 2 * P], U8, name="first_w2", tag="first_w2", align_bytes=64)
-        later_w2 = keep.tile([P, E, 2 * (N - P)], U8, name="later_w2", align_bytes=64)
-        nc.sync.dma_start(first_w2[:].bitcast(I32), w2_rows[:, :, : P // 2])
-        nc.sync.dma_start(later_w2[:].bitcast(I32), w2_rows[:, :, P // 2 :])
+        w2_sb = {}
+        for b0, b1 in W2_TILES:
+            columns = keep.tile([P, E, 2 * P * (b1 - b0)], U8, name=f"w2_from{b0}", align_bytes=64)
+            nc.sync.dma_start(columns[:].bitcast(I32), w2_rows[:, :, b0 * P // 2 : b1 * P // 2])
+            for b in range(b0, b1):
+                w2_sb[b] = columns[:, :, 2 * P * (b - b0) : 2 * P * (b - b0 + 1)]
         pos_sb = [keep.tile([P, T // LIST_ROWS], U16, name=f"pos_sb{r}") for r in range(2)]
         nc.sync.dma_start(pos_sb[0][:], pos1)
         nc.sync.dma_start(pos_sb[1][:], pos2)
@@ -214,10 +217,9 @@ def tile_moe_pln_glu_silu_kernel(
         y_sb = {}
 
         def second_product(target, b, e, c0, c1):
-            weights = first_w2[:, e, :] if b == 0 else later_w2[:, e, 2 * (b - 1) * P : 2 * b * P]
             nc.tensor.matmul_mx(
                 out=target,
-                lhsT=weights.bitcast(FP4X4),
+                lhsT=w2_sb[b][:, e, :].bitcast(FP4X4),
                 lhsT_scale=planes[2][:, e, b * P : (b + 1) * P],
                 rhs=h_codes[e][:, c0:c1].bitcast(FP8X4),
                 rhs_scale=h_scales[e][:, c0:c1],
@@ -236,7 +238,7 @@ def tile_moe_pln_glu_silu_kernel(
 
         def later_results(b, pair, copy):
             if pair == 0:
-                tag = ("y_sb0", "first_w2", "y_sb2", "y_sb0")[b]
+                tag = ("y_sb0", "w2_from0", "y_sb2", "y_sb0")[b]
                 y_sb[b] = keep.tile([P, S], F32, name=f"y_sb{b}", tag=tag, align_bytes=64)
             e0, e1 = EXPERT_PAIRS[pair]
             y_bank = bank([P, 2, C], LATER_BANKS[b][pair])
@@ -263,7 +265,7 @@ def tile_moe_pln_glu_silu_kernel(
 
         def pick(b, r, t0, t1):
             if b == 0:
-                picked[b, r] = keep.tile([P, T], F32, name="picked0", tag=f"h_codes{E - 1}", align_bytes=64)
+                picked[b, r] = keep.tile([P, T], F32, name="picked0", tag="w2_from1", align_bytes=64)
             elif t0 == 0:
                 picked[b, r] = work.tile([P, T], F32, name="picked")
             nc.scalar.activation(picked[b, r][:, t0:t1], y_sb[b][:].indirect(listed(r, t0, t1)), COPY)

@@ -37,10 +37,10 @@ TURN_BANKS = (6, 7, 5, 1, 2)
 FIRST_PIECES = tuple((units[0] * UNIT, (units[-1] + 1) * UNIT) for units in TURN_GROUPS)
 FIRST_BANKS = (0, 6, 7, 3, 4)
 FIRST_ON_VECTOR = (2,)
-EXPERT_PAIRS = ((1, 2), (0, 3))
-LATER_BANKS = {1: (5, 1), 2: (3, 4), 3: (5, 1)}
-GATE_BANKS = (4, 3)
-W2_TILES = ((0, 1), (1, 3), (3, 4))
+LATER_PIECES = {1: ((1,), (0, 3), (2,)), 2: ((1, 2), (0, 3)), 3: ((1, 2), (0, 3))}
+LATER_BANKS = {1: (5, 1, 3), 2: (4, 0), 3: (5, 1)}
+GATE_BANKS = (0, 4)
+W2_TILES = ((0, 3), (3, 4))
 LAST_CUTS = (0, 256, 384, T)
 
 FLOPS = 2 * S * (2 * K * H + H * N)
@@ -83,8 +83,6 @@ def tile_moe_pln_glu_silu_kernel(
         nc.sync.dma_start(offs_sb[:], offs)
 
         x_scales = keep.tile([P, T], U8, name="x_scales", align_bytes=64)
-        warm = keep.tile([P, 1], F32, name="warm")
-        nc.vector.memset(warm[:], 0.0)
         zero_planes(0)
         zero_planes(1)
         nc.vector.memset(x_scales[:].bitcast(I32), 0)
@@ -92,7 +90,6 @@ def tile_moe_pln_glu_silu_kernel(
         load_scales([nc.sync] * 4, 0, w1_scales)
         load_words(1, w3_words, 0, 1)
         load_scales([nc.sync] * 4, 1, w3_scales)
-        nc.scalar.activation(warm[:], warm[:], SILU)
         zero_planes(2)
         ident = keep.tile([P, P], F32, name="ident")
         nc.vector.memset(ident[:], 0.0)
@@ -196,7 +193,10 @@ def tile_moe_pln_glu_silu_kernel(
 
         def quantise(group):
             units, turned = TURN_GROUPS[group], turned_by_group[group]
-            hidden_k = work.tile([P, len(units) * UNIT * PACK], BF16, name="hidden_k", align_bytes=64)
+            if group == len(TURN_GROUPS) - 1:
+                hidden_k = keep.tile([P, UNIT * PACK], BF16, name="hidden_last", tag="y_sb1", align_bytes=64)
+            else:
+                hidden_k = work.tile([P, len(units) * UNIT * PACK], BF16, name="hidden_k", align_bytes=64)
             nc.scalar.copy(
                 hidden_k[:].bitcast(F32).rearrange("p (n s u) -> p n s u", u=2, s=UNIT),
                 turned[:].rearrange("p n u s -> p n s u"),
@@ -238,13 +238,14 @@ def tile_moe_pln_glu_silu_kernel(
 
         def later_results(b, pair, copy):
             if pair == 0:
-                tag = ("y_sb0", "w2_from0", "y_sb2", "y_sb0")[b]
+                tag = ("y_sb0", "y_sb1", "y_sb2", "y_sb0")[b]
                 y_sb[b] = keep.tile([P, S], F32, name=f"y_sb{b}", tag=tag, align_bytes=64)
-            e0, e1 = EXPERT_PAIRS[pair]
-            y_bank = bank([P, 2, C], LATER_BANKS[b][pair])
-            for n, e in enumerate((e0, e1)):
+            experts = LATER_PIECES[b][pair]
+            y_bank = bank([P, len(experts), C], LATER_BANKS[b][pair])
+            for n, e in enumerate(experts):
                 second_product(y_bank[:, n, :], b, e, 0, C)
-            copy(y_sb[b][:].rearrange("p (e c) -> p e c", c=C)[:, e0 : e1 + 1 : e1 - e0, :], y_bank[:])
+            columns = slice(experts[0], experts[-1] + 1, max(1, experts[-1] - experts[0]))
+            copy(y_sb[b][:].rearrange("p (e c) -> p e c", c=C)[:, columns, :], y_bank[:])
 
         parts = {(b, r): work.tile([P, T], F32, name="part") for b in range(BLOCKS) for r in range(2)}
         picked = {}
@@ -265,7 +266,7 @@ def tile_moe_pln_glu_silu_kernel(
 
         def pick(b, r, t0, t1):
             if b == 0:
-                picked[b, r] = keep.tile([P, T], F32, name="picked0", tag="w2_from1", align_bytes=64)
+                picked[b, r] = keep.tile([P, T], F32, name="picked0", tag="w2_from0", align_bytes=64)
             elif t0 == 0:
                 picked[b, r] = work.tile([P, T], F32, name="picked")
             nc.scalar.activation(picked[b, r][:, t0:t1], y_sb[b][:].indirect(listed(r, t0, t1)), COPY)
@@ -279,18 +280,23 @@ def tile_moe_pln_glu_silu_kernel(
             nc.sync.dma_start(out[b * P : (b + 1) * P, t0:t1], total[:])
 
         first_results()
+        later_results(1, 0, nc.vector.tensor_copy)
         pick_gated(0)
-        for b in (1, 2):
-            later_results(b, 0, nc.scalar.copy)
-            later_results(b, 1, nc.scalar.copy)
-            pick_gated(b)
+        later_results(1, 1, nc.scalar.copy)
+        later_results(1, 2, nc.scalar.copy)
+        pick_gated(1)
+        later_results(2, 0, nc.scalar.copy)
+        later_results(2, 1, nc.scalar.copy)
+        pick_gated(2)
         spread_gate(1)
         for b in (0, 1, 2):
             pick(b, 1, 0, T)
             weigh(b, 1, 0, T)
             if b < 2:
                 add_and_store(nc.gpsimd, b, 0, T)
-                later_results(3, b, nc.vector.tensor_copy)
+            if b == 0:
+                later_results(3, 0, nc.vector.tensor_copy)
+                later_results(3, 1, nc.vector.tensor_copy)
         spread_gate(0)
         t0, t1, t2, t3 = LAST_CUTS
         pick(3, 0, t0, t1)
@@ -299,8 +305,8 @@ def tile_moe_pln_glu_silu_kernel(
         pick(3, 1, t1, t2)
         pick(3, 1, t2, t3)
         weigh(3, 0, t0, t1)
-        add_and_store(nc.vector, 2, 0, T)
         weigh(3, 1, t0, t1)
+        add_and_store(nc.vector, 2, 0, T)
         weigh(3, 0, t1, t3)
         add_and_store(nc.vector, 3, t0, t1)
         weigh(3, 1, t1, t2)

@@ -27,6 +27,7 @@ LIST_ROWS = 16
 
 X_CUTS = (0, 256, T)
 SCALAR_EIGHTHS = 3
+LINE = 4
 GATHER_CUTS = (0, 128, 256, 640, 1024)
 UNIT_RUNS = ((0, 1), (2, 3, 4), (5, 6, 7))
 ON_GPSIMD = (0, 1)
@@ -37,10 +38,10 @@ TURN_BANKS = (6, 7, 5, 1, 2)
 FIRST_PIECES = tuple((units[0] * UNIT, (units[-1] + 1) * UNIT) for units in TURN_GROUPS)
 FIRST_BANKS = (0, 6, 7, 3, 4)
 FIRST_ON_VECTOR = (2,)
-LATER_PIECES = {1: ((1,), (0, 3), (2,)), 2: ((1, 2), (0, 3)), 3: ((1, 2), (0, 3))}
-LATER_BANKS = {1: (5, 1, 3), 2: (4, 0), 3: (5, 1)}
-GATE_BANKS = (0, 4)
-W2_TILES = ((0, 3), (3, 4))
+LATER_PIECES = {1: ((1, 2), (0, 3)), 2: ((1,), (0, 3), (2,)), 3: ((1, 2), (0, 3))}
+LATER_BANKS = {1: (5, 2), 2: (1, 3, 4), 3: (5, 2)}
+GATE_BANKS = (4, 3)
+W2_TILES = ((0, 1), (1, 3), (3, 4))
 LAST_CUTS = (0, 256, 384, T)
 
 FLOPS = 2 * S * (2 * K * H + H * N)
@@ -118,10 +119,11 @@ def tile_moe_pln_glu_silu_kernel(
         x_codes = keep.tile([P, T], U32, name="x_codes", tag="x_codes", align_bytes=64)
         for raw, (t0, t1) in zip(x_raw, pieces):
             x_bf = rounding.tile([P, t1 - t0, PACK], BF16, name="x_bf", align_bytes=64)
-            source = raw[:].rearrange("p j t -> p t j")
-            share = (t1 - t0) * SCALAR_EIGHTHS // 8
-            nc.scalar.copy(x_bf[:, :share, :], source[:, :share, :])
-            nc.vector.tensor_copy(x_bf[:, share:, :], source[:, share:, :])
+            source = raw[:].rearrange("p j (c i) -> p c j i", i=LINE)
+            target = x_bf[:].rearrange("p (c i) j -> p c j i", i=LINE)
+            share = (t1 - t0) * SCALAR_EIGHTHS // 8 // LINE
+            nc.scalar.copy(target[:, :share], source[:, :share])
+            nc.vector.tensor_copy(target[:, share:], source[:, share:])
             tokens = slice(t0, t1)
             nc.vector.quantize_mx(
                 out=x_codes[:, tokens].bitcast(FP8X4),
@@ -194,7 +196,7 @@ def tile_moe_pln_glu_silu_kernel(
         def quantise(group):
             units, turned = TURN_GROUPS[group], turned_by_group[group]
             if group == len(TURN_GROUPS) - 1:
-                hidden_k = keep.tile([P, UNIT * PACK], BF16, name="hidden_last", tag="y_sb1", align_bytes=64)
+                hidden_k = keep.tile([P, UNIT * PACK], BF16, name="hidden_last", tag="y_sb2", align_bytes=64)
             else:
                 hidden_k = work.tile([P, len(units) * UNIT * PACK], BF16, name="hidden_k", align_bytes=64)
             nc.scalar.copy(
@@ -238,7 +240,7 @@ def tile_moe_pln_glu_silu_kernel(
 
         def later_results(b, pair, copy):
             if pair == 0:
-                tag = ("y_sb0", "y_sb1", "y_sb2", "y_sb0")[b]
+                tag = ("y_sb0", "w2_from0", "y_sb2", "y_sb0")[b]
                 y_sb[b] = keep.tile([P, S], F32, name=f"y_sb{b}", tag=tag, align_bytes=64)
             experts = LATER_PIECES[b][pair]
             y_bank = bank([P, len(experts), C], LATER_BANKS[b][pair])
@@ -266,7 +268,7 @@ def tile_moe_pln_glu_silu_kernel(
 
         def pick(b, r, t0, t1):
             if b == 0:
-                picked[b, r] = keep.tile([P, T], F32, name="picked0", tag="w2_from0", align_bytes=64)
+                picked[b, r] = keep.tile([P, T], F32, name="picked0", tag="w2_from1", align_bytes=64)
             elif t0 == 0:
                 picked[b, r] = work.tile([P, T], F32, name="picked")
             nc.scalar.activation(picked[b, r][:, t0:t1], y_sb[b][:].indirect(listed(r, t0, t1)), COPY)
@@ -280,13 +282,13 @@ def tile_moe_pln_glu_silu_kernel(
             nc.sync.dma_start(out[b * P : (b + 1) * P, t0:t1], total[:])
 
         first_results()
-        later_results(1, 0, nc.vector.tensor_copy)
+        later_results(2, 0, nc.vector.tensor_copy)
         pick_gated(0)
+        later_results(1, 0, nc.scalar.copy)
         later_results(1, 1, nc.scalar.copy)
-        later_results(1, 2, nc.scalar.copy)
         pick_gated(1)
-        later_results(2, 0, nc.scalar.copy)
         later_results(2, 1, nc.scalar.copy)
+        later_results(2, 2, nc.scalar.copy)
         pick_gated(2)
         spread_gate(1)
         for b in (0, 1, 2):

@@ -25,24 +25,25 @@ UNITS_PER_EXPERT = C // UNIT
 BLOCKS = N // P
 LIST_ROWS = 16
 
+LINE = 4
+
 X_CUTS = (0, 256, T)
 SCALAR_EIGHTHS = 3
-LINE = 4
 GATHER_CUTS = (0, 128, 256, 640, 1024)
-UNIT_RUNS = ((0, 1), (2, 3, 4), (5, 6, 7))
+EARLY_RUNS = ((0, 1), (2, 3, 4))
 ON_GPSIMD = (0, 1)
-A_BANKS = (0, 1, 4, 5, 0, 4, 5, 0)
-B_BANKS = (2, 3, 6, 7, 1, 2, 3, 4)
 TURN_GROUPS = ((2, 3), (4, 5), (0, 1), (6,), (7,))
-TURN_BANKS = (6, 7, 5, 1, 2)
 FIRST_PIECES = tuple((units[0] * UNIT, (units[-1] + 1) * UNIT) for units in TURN_GROUPS)
-FIRST_BANKS = (0, 6, 7, 3, 4)
 FIRST_ON_VECTOR = (2,)
-LATER_PIECES = {1: ((1, 2), (0, 3)), 2: ((1,), (0, 3), (2,)), 3: ((1, 2), (0, 3))}
-LATER_BANKS = {1: (5, 2), 2: (1, 3, 4), 3: (5, 2)}
-GATE_BANKS = (4, 3)
+LATER_PIECES = {1: ((1, 2), (3, 0)), 2: ((1,), (3, 0), (2,)), 3: ((1, 2), (3, 0))}
 W2_TILES = ((0, 1), (1, 3), (3, 4))
 LAST_CUTS = (0, 256, 384, T)
+
+A_BANKS = (0, 1, 4, 5, 0, 4, 5, 4)
+B_BANKS = (2, 3, 6, 7, 1, 2, 7, 1)
+TURN_BANKS = (0, 6, 5, 7, 1)
+LATER_BANKS = {1: (3, 0), 2: (2, 6, 2), 3: (4, 3)}
+GATE_BANKS = (2, 0)
 
 FLOPS = 2 * S * (2 * K * H + H * N)
 
@@ -71,10 +72,10 @@ def tile_moe_pln_glu_silu_kernel(
                 words[m][:, e0:e1, :].bitcast(I32), dram.bitcast(I32)[e0:e1].rearrange("e o p i -> p (e o) i")
             )
 
-        def load_scales(engines, m, dram):
+        def load_scales(m, dram):
             rows = dram.bitcast(I32).rearrange("e o (Q r) i -> r Q (e o) i", r=4)
-            for r, engine in enumerate(engines):
-                engine.dma_start(planes[m][:].bitcast(I32)[r : P : 32], rows[r])
+            for r in range(4):
+                nc.sync.dma_start(planes[m][:].bitcast(I32)[r : P : 32], rows[r])
 
         pieces = list(zip(X_CUTS[:-1], X_CUTS[1:]))
         x_raw = [keep.tile([P, PACK, t1 - t0], F32, name=f"x_raw{t0}", align_bytes=64) for t0, t1 in pieces]
@@ -88,9 +89,9 @@ def tile_moe_pln_glu_silu_kernel(
         zero_planes(1)
         nc.vector.memset(x_scales[:].bitcast(I32), 0)
         load_words(0, w1_words, 0, 1)
-        load_scales([nc.sync] * 4, 0, w1_scales)
+        load_scales(0, w1_scales)
         load_words(1, w3_words, 0, 1)
-        load_scales([nc.sync] * 4, 1, w3_scales)
+        load_scales(1, w3_scales)
         zero_planes(2)
         ident = keep.tile([P, P], F32, name="ident")
         nc.vector.memset(ident[:], 0.0)
@@ -98,7 +99,7 @@ def tile_moe_pln_glu_silu_kernel(
         load_words(0, w1_words, 1, 2)
         load_words(0, w1_words, 2, E)
         load_words(1, w3_words, 1, E)
-        load_scales([nc.sync] * 4, 2, w2_scales)
+        load_scales(2, w2_scales)
         w2_rows = w2_words.bitcast(I32).rearrange("e o p i -> p (e o) i")
         w2_sb = {}
         for b0, b1 in W2_TILES:
@@ -168,7 +169,10 @@ def tile_moe_pln_glu_silu_kernel(
 
         def activate(unit):
             first_product(a_banks, A_BANKS, 0, unit)
-            act[unit] = work.tile([P, H], F32, name="act")
+            if unit == UNITS - 1:
+                act[unit] = keep.tile([P, H], F32, name="act_last", tag="hidden_early")
+            else:
+                act[unit] = work.tile([P, H], F32, name="act")
             nc.scalar.activation(paired(act[unit]), by_pair(a_banks[unit]), SILU)
 
         def multiply(unit):
@@ -179,7 +183,12 @@ def tile_moe_pln_glu_silu_kernel(
                 hidden[unit] = held[:, ON_GPSIMD.index(unit), :]
                 nc.gpsimd.tensor_tensor(hidden[unit], act[unit][:], up[:], MULT)
             else:
-                hidden[unit] = work.tile([P, H], BF16, name="hidden")
+                if unit == TURN_GROUPS[0][-1]:
+                    hidden[unit] = keep.tile([P, H], BF16, name="hidden_early")
+                elif unit == UNITS - 1:
+                    hidden[unit] = keep.tile([P, H], BF16, name="hidden_late", tag="y_sb0", align_bytes=64)
+                else:
+                    hidden[unit] = work.tile([P, H], BF16, name="hidden")
                 nc.vector.tensor_tensor(paired(hidden[unit]), paired(act[unit]), by_pair(b_banks[unit]), MULT)
 
         turned_by_group = {}
@@ -193,7 +202,9 @@ def tile_moe_pln_glu_silu_kernel(
                     nc.tensor.transpose(turned[:, n, u, :], pairs[:, u * P : (u + 1) * P], ident[:])
             turned_by_group[group] = turned
 
-        def quantise(group):
+        hidden_by_group = {}
+
+        def turn_out(group):
             units, turned = TURN_GROUPS[group], turned_by_group[group]
             if group == len(TURN_GROUPS) - 1:
                 hidden_k = keep.tile([P, UNIT * PACK], BF16, name="hidden_last", tag="y_sb2", align_bytes=64)
@@ -203,20 +214,36 @@ def tile_moe_pln_glu_silu_kernel(
                 hidden_k[:].bitcast(F32).rearrange("p (n s u) -> p n s u", u=2, s=UNIT),
                 turned[:].rearrange("p n u s -> p n s u"),
             )
+            hidden_by_group[group] = hidden_k
+
+        def quantise(group):
+            units, hidden_k = TURN_GROUPS[group], hidden_by_group[group]
             e, s0 = units[0] // UNITS_PER_EXPERT, units[0] % UNITS_PER_EXPERT * UNIT
             slots = slice(s0, s0 + len(units) * UNIT)
             nc.vector.quantize_mx(out=h_codes[e][:, slots].bitcast(FP8X4), scales=h_scales[e][:, slots], in_=hidden_k[:])
 
-        for run in UNIT_RUNS:
+        for run in EARLY_RUNS:
             for stage in (activate, multiply):
                 for unit in run:
                     stage(unit)
-        for group in range(len(TURN_GROUPS)):
+        third_last, second_last, last = range(UNITS - 3, UNITS)
+        activate(third_last)
+        activate(second_last)
+        multiply(third_last)
+        turn(0)
+        turn_out(0)
+        multiply(second_last)
+        quantise(0)
+        activate(last)
+        multiply(last)
+        for group in range(1, len(TURN_GROUPS)):
             turn(group)
-        for group in range(len(TURN_GROUPS)):
+        for group in range(1, len(TURN_GROUPS)):
+            turn_out(group)
             quantise(group)
 
         y_sb = {}
+        later_tags = {1: "w2_from0", 2: "y_sb2", 3: "y_sb0"}
 
         def second_product(target, b, e, c0, c1):
             nc.tensor.matmul_mx(
@@ -232,21 +259,21 @@ def tile_moe_pln_glu_silu_kernel(
         def first_results():
             y_sb[0] = keep.tile([P, S], F32, name="y_sb0", align_bytes=64)
             for piece, (s0, s1) in enumerate(FIRST_PIECES):
-                y_bank = bank([P, s1 - s0], FIRST_BANKS[piece])
+                y_bank = bank([P, s1 - s0], TURN_BANKS[piece])
                 e = s0 // C
                 second_product(y_bank[:], 0, e, s0 - e * C, s1 - e * C)
                 copy = nc.vector.tensor_copy if piece in FIRST_ON_VECTOR else nc.scalar.copy
                 copy(y_sb[0][:, s0:s1], y_bank[:])
 
-        def later_results(b, pair, copy):
-            if pair == 0:
-                tag = ("y_sb0", "w2_from0", "y_sb2", "y_sb0")[b]
-                y_sb[b] = keep.tile([P, S], F32, name=f"y_sb{b}", tag=tag, align_bytes=64)
-            experts = LATER_PIECES[b][pair]
-            y_bank = bank([P, len(experts), C], LATER_BANKS[b][pair])
-            for n, e in enumerate(experts):
-                second_product(y_bank[:, n, :], b, e, 0, C)
-            columns = slice(experts[0], experts[-1] + 1, max(1, experts[-1] - experts[0]))
+        def later_results(b, piece, copy):
+            if piece == 0:
+                y_sb[b] = keep.tile([P, S], F32, name=f"y_sb{b}", tag=later_tags[b], align_bytes=64)
+            experts = LATER_PIECES[b][piece]
+            y_bank = bank([P, len(experts), C], LATER_BANKS[b][piece])
+            low, high = min(experts), max(experts)
+            for e in experts:
+                second_product(y_bank[:, 0 if e == low else 1, :], b, e, 0, C)
+            columns = slice(low, high + 1, max(1, high - low))
             copy(y_sb[b][:].rearrange("p (e c) -> p e c", c=C)[:, columns, :], y_bank[:])
 
         parts = {(b, r): work.tile([P, T], F32, name="part") for b in range(BLOCKS) for r in range(2)}

@@ -35,14 +35,14 @@ ON_GPSIMD = (0, 1)
 TURN_GROUPS = ((2, 3), (4, 5), (0, 1), (6,), (7,))
 FIRST_PIECES = tuple((units[0] * UNIT, (units[-1] + 1) * UNIT) for units in TURN_GROUPS)
 FIRST_ON_VECTOR = (2,)
-LATER_PIECES = {1: ((1, 2), (3, 0)), 2: ((1,), (3, 0), (2,)), 3: ((1, 2), (3, 0))}
+LATER_PIECES = {1: ((1, 2), (3, 0)), 2: ((1,), (3, 0), (2,)), 3: ((3, 0), (1, 2))}
 W2_TILES = ((0, 1), (1, 3), (3, 4))
 LAST_CUTS = (0, 256, 384, T)
 
 A_BANKS = (0, 1, 4, 5, 0, 4, 5, 4)
 B_BANKS = (2, 3, 6, 7, 1, 2, 7, 1)
 TURN_BANKS = (0, 6, 5, 7, 1)
-LATER_BANKS = {1: (3, 0), 2: (2, 6, 2), 3: (4, 3)}
+LATER_BANKS = {1: (3, 0), 2: (2, 6, 2), 3: (3, 4)}
 GATE_BANKS = (2, 0)
 
 FLOPS = 2 * S * (2 * K * H + H * N)
@@ -55,6 +55,7 @@ def tile_moe_pln_glu_silu_kernel(
     with ExitStack() as ctx:
         keep = ctx.enter_context(tc.tile_pool(name="keep", bufs=1))
         rounding = ctx.enter_context(tc.tile_pool(name="rounding", bufs=2))
+        late = ctx.enter_context(tc.tile_pool(name="late", bufs=1))
         work = ctx.enter_context(tc.tile_pool(name="work", bufs=8))
         psum = ctx.enter_context(tc.psum_pool(name="psum", bufs=1))
 
@@ -207,7 +208,7 @@ def tile_moe_pln_glu_silu_kernel(
         def turn_out(group):
             units, turned = TURN_GROUPS[group], turned_by_group[group]
             if group == len(TURN_GROUPS) - 1:
-                hidden_k = keep.tile([P, UNIT * PACK], BF16, name="hidden_last", tag="y_sb2", align_bytes=64)
+                hidden_k = late.tile([P, UNIT * PACK], BF16, name="hidden_last", align_bytes=64, offset=4 * S - UNIT * PACK)
             else:
                 hidden_k = work.tile([P, len(units) * UNIT * PACK], BF16, name="hidden_k", align_bytes=64)
             nc.scalar.copy(
@@ -243,7 +244,6 @@ def tile_moe_pln_glu_silu_kernel(
             quantise(group)
 
         y_sb = {}
-        later_tags = {1: "w2_from0", 2: "y_sb2", 3: "y_sb0"}
 
         def second_product(target, b, e, c0, c1):
             nc.tensor.matmul_mx(
@@ -266,8 +266,10 @@ def tile_moe_pln_glu_silu_kernel(
                 copy(y_sb[0][:, s0:s1], y_bank[:])
 
         def later_results(b, piece, copy):
-            if piece == 0:
-                y_sb[b] = keep.tile([P, S], F32, name=f"y_sb{b}", tag=later_tags[b], align_bytes=64)
+            if piece == 0 and b == 3:
+                y_sb[b] = keep.tile([P, S], F32, name="y_sb3", tag="y_sb0", align_bytes=64)
+            elif piece == 0:
+                y_sb[b] = late.tile([P, S], F32, name=f"y_sb{b}", align_bytes=64, offset=4 * S * (b - 1))
             experts = LATER_PIECES[b][piece]
             y_bank = bank([P, len(experts), C], LATER_BANKS[b][piece])
             low, high = min(experts), max(experts)
@@ -310,8 +312,8 @@ def tile_moe_pln_glu_silu_kernel(
 
         first_results()
         later_results(2, 0, nc.vector.tensor_copy)
+        later_results(1, 0, nc.vector.tensor_copy)
         pick_gated(0)
-        later_results(1, 0, nc.scalar.copy)
         later_results(1, 1, nc.scalar.copy)
         pick_gated(1)
         later_results(2, 1, nc.scalar.copy)
@@ -325,7 +327,8 @@ def tile_moe_pln_glu_silu_kernel(
                 add_and_store(nc.gpsimd, b, 0, T)
             if b == 0:
                 later_results(3, 0, nc.vector.tensor_copy)
-                later_results(3, 1, nc.vector.tensor_copy)
+            if b == 1:
+                later_results(3, 1, nc.scalar.copy)
         spread_gate(0)
         t0, t1, t2, t3 = LAST_CUTS
         pick(3, 0, t0, t1)

@@ -35,14 +35,14 @@ ON_GPSIMD = (0, 1)
 TURN_GROUPS = ((2, 3), (4, 5), (0, 1), (6,), (7,))
 FIRST_PIECES = tuple((units[0] * UNIT, (units[-1] + 1) * UNIT) for units in TURN_GROUPS)
 FIRST_ON_VECTOR = (2,)
-LATER_PIECES = {1: ((1, 2), (3, 0)), 2: ((1,), (3, 0), (2,)), 3: ((3, 0), (1, 2))}
+LATER_PIECES = {1: ((1, 2), (3, 0)), 2: ((1,), (3, 0), (2,)), 3: ((1, 2), (3, 0))}
 W2_TILES = ((0, 1), (1, 3), (3, 4))
 LAST_CUTS = (0, 256, 384, T)
 
 A_BANKS = (0, 1, 4, 5, 0, 4, 5, 4)
 B_BANKS = (2, 3, 6, 7, 1, 2, 7, 1)
 TURN_BANKS = (0, 6, 5, 7, 1)
-LATER_BANKS = {1: (3, 0), 2: (2, 6, 2), 3: (3, 4)}
+LATER_BANKS = {1: (3, 0), 2: (2, 6, 2), 3: (4, 6)}
 GATE_BANKS = (2, 0)
 
 FLOPS = 2 * S * (2 * K * H + H * N)
@@ -187,7 +187,7 @@ def tile_moe_pln_glu_silu_kernel(
                 if unit == TURN_GROUPS[0][-1]:
                     hidden[unit] = keep.tile([P, H], BF16, name="hidden_early")
                 elif unit == UNITS - 1:
-                    hidden[unit] = keep.tile([P, H], BF16, name="hidden_late", tag="y_sb0", align_bytes=64)
+                    hidden[unit] = keep.tile([P, H], BF16, name="hidden_late", tag="y_sb3", align_bytes=64)
                 else:
                     hidden[unit] = work.tile([P, H], BF16, name="hidden")
                 nc.vector.tensor_tensor(paired(hidden[unit]), paired(act[unit]), by_pair(b_banks[unit]), MULT)
@@ -208,7 +208,9 @@ def tile_moe_pln_glu_silu_kernel(
         def turn_out(group):
             units, turned = TURN_GROUPS[group], turned_by_group[group]
             if group == len(TURN_GROUPS) - 1:
-                hidden_k = late.tile([P, UNIT * PACK], BF16, name="hidden_last", align_bytes=64, offset=4 * S - UNIT * PACK)
+                hidden_k = late.tile([P, UNIT * PACK], BF16, name="hidden_last", align_bytes=64, offset=0)
+            elif group == 2:
+                hidden_k = late.tile([P, C * PACK], BF16, name="hidden_third", align_bytes=64, offset=4 * S)
             else:
                 hidden_k = work.tile([P, len(units) * UNIT * PACK], BF16, name="hidden_k", align_bytes=64)
             nc.scalar.copy(
@@ -264,10 +266,12 @@ def tile_moe_pln_glu_silu_kernel(
                 second_product(y_bank[:], 0, e, s0 - e * C, s1 - e * C)
                 copy = nc.vector.tensor_copy if piece in FIRST_ON_VECTOR else nc.scalar.copy
                 copy(y_sb[0][:, s0:s1], y_bank[:])
+                if piece == 1:
+                    later_results(3, 0, nc.scalar.copy)
 
         def later_results(b, piece, copy):
             if piece == 0 and b == 3:
-                y_sb[b] = keep.tile([P, S], F32, name="y_sb3", tag="y_sb0", align_bytes=64)
+                y_sb[b] = keep.tile([P, S], F32, name="y_sb3", align_bytes=64)
             elif piece == 0:
                 y_sb[b] = late.tile([P, S], F32, name=f"y_sb{b}", align_bytes=64, offset=4 * S * (b - 1))
             experts = LATER_PIECES[b][piece]
@@ -296,9 +300,7 @@ def tile_moe_pln_glu_silu_kernel(
             nc.vector.tensor_tensor(parts[b, 0][:], y_sb[b][:].indirect(listed(0, 0, T)), first_gate[:], MULT)
 
         def pick(b, r, t0, t1):
-            if b == 0:
-                picked[b, r] = keep.tile([P, T], F32, name="picked0", tag="w2_from1", align_bytes=64)
-            elif t0 == 0:
+            if t0 == 0:
                 picked[b, r] = work.tile([P, T], F32, name="picked")
             nc.scalar.activation(picked[b, r][:, t0:t1], y_sb[b][:].indirect(listed(r, t0, t1)), COPY)
 
@@ -313,22 +315,23 @@ def tile_moe_pln_glu_silu_kernel(
         first_results()
         later_results(2, 0, nc.vector.tensor_copy)
         later_results(1, 0, nc.vector.tensor_copy)
+        later_results(2, 2, nc.vector.tensor_copy)
         pick_gated(0)
         later_results(1, 1, nc.scalar.copy)
         pick_gated(1)
-        later_results(2, 1, nc.scalar.copy)
-        later_results(2, 2, nc.scalar.copy)
-        pick_gated(2)
         spread_gate(1)
-        for b in (0, 1, 2):
-            pick(b, 1, 0, T)
-            weigh(b, 1, 0, T)
-            if b < 2:
-                add_and_store(nc.gpsimd, b, 0, T)
-            if b == 0:
-                later_results(3, 0, nc.vector.tensor_copy)
-            if b == 1:
-                later_results(3, 1, nc.scalar.copy)
+        pick(0, 1, 0, T)
+        weigh(0, 1, 0, T)
+        add_and_store(nc.gpsimd, 0, 0, T)
+        later_results(2, 1, nc.scalar.copy)
+        pick_gated(2)
+        later_results(3, 1, nc.vector.tensor_copy)
+        pick(1, 1, 0, T)
+        weigh(1, 1, 0, T)
+        pick(2, 1, 0, T)
+        weigh(2, 1, 0, T)
+        add_and_store(nc.vector, 1, 0, T)
+        add_and_store(nc.gpsimd, 2, 0, T)
         spread_gate(0)
         t0, t1, t2, t3 = LAST_CUTS
         pick(3, 0, t0, t1)
@@ -338,7 +341,6 @@ def tile_moe_pln_glu_silu_kernel(
         pick(3, 1, t2, t3)
         weigh(3, 0, t0, t1)
         weigh(3, 1, t0, t1)
-        add_and_store(nc.vector, 2, 0, T)
         weigh(3, 0, t1, t3)
         add_and_store(nc.vector, 3, t0, t1)
         weigh(3, 1, t1, t2)

@@ -315,7 +315,6 @@ def tile_moe_pln_glu_silu_kernel(
         first_results()
         later_results(2, 0, nc.vector.tensor_copy)
         later_results(1, 0, nc.vector.tensor_copy)
-        later_results(2, 2, nc.vector.tensor_copy)
         pick_gated(0)
         later_results(1, 1, nc.scalar.copy)
         pick_gated(1)
@@ -324,6 +323,7 @@ def tile_moe_pln_glu_silu_kernel(
         weigh(0, 1, 0, T)
         add_and_store(nc.gpsimd, 0, 0, T)
         later_results(2, 1, nc.scalar.copy)
+        later_results(2, 2, nc.scalar.copy)
         pick_gated(2)
         later_results(3, 1, nc.vector.tensor_copy)
         pick(1, 1, 0, T)

@@ -82,8 +82,9 @@ def tile_moe_pln_glu_silu_kernel(
         x_raw = [keep.tile([P, PACK, t1 - t0], F32, name=f"x_raw{t0}", align_bytes=64) for t0, t1 in pieces]
         for raw, (t0, t1) in zip(x_raw, pieces):
             nc.sync.dma_start(raw[:], xT.rearrange("(p j) t -> p j t", j=PACK)[:, :, t0:t1])
-        offs_sb = keep.tile([P, S // LIST_ROWS], U16, name="offs_sb")
-        nc.sync.dma_start(offs_sb[:], offs)
+            if t0 == 0:
+                offs_sb = keep.tile([P, S // LIST_ROWS], U16, name="offs_sb")
+                nc.sync.dma_start(offs_sb[:], offs)
 
         x_scales = keep.tile([P, T], U8, name="x_scales", align_bytes=64)
         zero_planes(0)
@@ -124,14 +125,17 @@ def tile_moe_pln_glu_silu_kernel(
             source = raw[:].rearrange("p j (c i) -> p c j i", i=LINE)
             target = x_bf[:].rearrange("p (c i) j -> p c j i", i=LINE)
             share = (t1 - t0) * SCALAR_EIGHTHS // 8 // LINE
+            middle = (t1 - t0) // 2
             nc.scalar.copy(target[:, :share], source[:, :share])
-            nc.vector.tensor_copy(target[:, share:], source[:, share:])
-            tokens = slice(t0, t1)
-            nc.vector.quantize_mx(
-                out=x_codes[:, tokens].bitcast(FP8X4),
-                scales=x_scales[:, tokens],
-                in_=x_bf[:].rearrange("p t j -> p (t j)"),
-            )
+            nc.vector.tensor_copy(target[:, middle // LINE :], source[:, middle // LINE :])
+            nc.vector.tensor_copy(target[:, share : middle // LINE], source[:, share : middle // LINE])
+            for c0 in (middle, 0):
+                tokens = slice(t0 + c0, t0 + c0 + middle)
+                nc.vector.quantize_mx(
+                    out=x_codes[:, tokens].bitcast(FP8X4),
+                    scales=x_scales[:, tokens],
+                    in_=x_bf[:, c0 : c0 + middle, :].rearrange("p t j -> p (t j)"),
+                )
 
         slot_codes, slot_scales = {}, {}
         for cut, (s0, s1) in enumerate(zip(GATHER_CUTS[:-1], GATHER_CUTS[1:])):

from contextlib import ExitStack

import concourse.mybir as mybir
from concourse.masks import make_identity

F32 = mybir.dt.float32
BF16 = mybir.dt.bfloat16
I32 = mybir.dt.int32
U32 = mybir.dt.uint32
U16 = mybir.dt.uint16
U8 = mybir.dt.uint8
FP8X4 = mybir.dt.float8_e4m3fn_x4
FP4X4 = mybir.dt.float4_e2m1fn_x4
ADD, MULT = mybir.AluOpType.add, mybir.AluOpType.mult
SILU = mybir.ActivationFunctionType.Silu
COPY = mybir.ActivationFunctionType.Copy

P = 128
K, T, E, C, H, N = 512, 512, 4, 256, 512, 512
S = E * C
PACK = 4
UNIT = 128
UNITS = S // UNIT
UNITS_PER_EXPERT = C // UNIT
BLOCKS = N // P
LIST_ROWS = 16

LINE = 4

X_CUTS = (0, 256, T)
SCALAR_EIGHTHS = 3
GATHER_CUTS = (0, 128, 256, 640, 1024)
EARLY_RUNS = ((0, 1), (2, 3, 4))
ON_GPSIMD = (0, 1)
TURN_GROUPS = ((2, 3), (4, 5), (0, 1), (6,), (7,))
FIRST_PIECES = tuple((units[0] * UNIT, (units[-1] + 1) * UNIT) for units in TURN_GROUPS)
FIRST_ON_VECTOR = (2,)
LATER_PIECES = {1: ((1, 2), (3, 0)), 2: ((1,), (3, 0), (2,)), 3: ((1, 2), (3, 0))}
W2_TILES = ((0, 1), (1, 3), (3, 4))
LAST_CUTS = (0, 256, 384, T)

A_BANKS = (0, 1, 4, 5, 0, 4, 5, 4)
B_BANKS = (2, 3, 6, 7, 1, 2, 7, 1)
TURN_BANKS = (0, 6, 5, 7, 1)
LATER_BANKS = {1: (3, 0), 2: (2, 6, 2), 3: (4, 6)}
GATE_BANKS = (2, 0)

FLOPS = 2 * S * (2 * K * H + H * N)


def tile_moe_pln_glu_silu_kernel(
    tc, xT, w1_words, w1_scales, w3_words, w3_scales, w2_words, w2_scales, gate, offs, pos1, pos2, out
):
    nc = tc.nc
    with ExitStack() as ctx:
        keep = ctx.enter_context(tc.tile_pool(name="keep", bufs=1))
        rounding = ctx.enter_context(tc.tile_pool(name="rounding", bufs=2))
        late = ctx.enter_context(tc.tile_pool(name="late", bufs=1))
        work = ctx.enter_context(tc.tile_pool(name="work", bufs=8))
        psum = ctx.enter_context(tc.psum_pool(name="psum", bufs=1))

        def bank(shape, number):
            return psum.tile(shape, F32, name=f"bank{number}")

        words = [keep.tile([P, E, 2 * H], U8, name=f"words{m}", align_bytes=64) for m in range(2)]
        planes = [keep.tile([P, E, H], U8, name=f"planes{m}", align_bytes=64) for m in range(3)]

        def zero_planes(m):
            nc.vector.memset(planes[m][:].rearrange("p e i -> p (e i)").bitcast(I32), 0)

        def load_words(m, dram, e0, e1):
            nc.sync.dma_start(
                words[m][:, e0:e1, :].bitcast(I32), dram.bitcast(I32)[e0:e1].rearrange("e o p i -> p (e o) i")
            )

        def load_scales(m, dram):
            rows = dram.bitcast(I32).rearrange("e o (Q r) i -> r Q (e o) i", r=4)
            for r in range(4):
                nc.sync.dma_start(planes[m][:].bitcast(I32)[r : P : 32], rows[r])

        pieces = list(zip(X_CUTS[:-1], X_CUTS[1:]))
        x_raw = [keep.tile([P, PACK, t1 - t0], F32, name=f"x_raw{t0}", align_bytes=64) for t0, t1 in pieces]
        for raw, (t0, t1) in zip(x_raw, pieces):
            nc.sync.dma_start(raw[:], xT.rearrange("(p j) t -> p j t", j=PACK)[:, :, t0:t1])
            if t0 == 0:
                offs_sb = keep.tile([P, S // LIST_ROWS], U16, name="offs_sb")
                nc.sync.dma_start(offs_sb[:], offs)

        x_scales = keep.tile([P, T], U8, name="x_scales", align_bytes=64)
        zero_planes(0)
        zero_planes(1)
        nc.vector.memset(x_scales[:].bitcast(I32), 0)
        load_words(0, w1_words, 0, 1)
        load_scales(0, w1_scales)
        load_words(1, w3_words, 0, 1)
        load_scales(1, w3_scales)
        zero_planes(2)
        ident = keep.tile([P, P], F32, name="ident")
        nc.vector.memset(ident[:], 0.0)
        make_identity(nc, ident[:], nomemset=True)
        load_words(0, w1_words, 1, 2)
        load_words(0, w1_words, 2, E)
        load_words(1, w3_words, 1, E)
        load_scales(2, w2_scales)
        w2_rows = w2_words.bitcast(I32).rearrange("e o p i -> p (e o) i")
        w2_sb = {}
        for b0, b1 in W2_TILES:
            columns = keep.tile([P, E, 2 * P * (b1 - b0)], U8, name=f"w2_from{b0}", align_bytes=64)
            nc.sync.dma_start(columns[:].bitcast(I32), w2_rows[:, :, b0 * P // 2 : b1 * P // 2])
            for b in range(b0, b1):
                w2_sb[b] = columns[:, :, 2 * P * (b - b0) : 2 * P * (b - b0 + 1)]
        pos_sb = [keep.tile([P, T // LIST_ROWS], U16, name=f"pos_sb{r}") for r in range(2)]
        nc.sync.dma_start(pos_sb[0][:], pos1)
        nc.sync.dma_start(pos_sb[1][:], pos2)
        first_gate = keep.tile([P, T], F32, name="first_gate")
        nc.sync.dma_start(first_gate[:], gate[0, :P, :])
        gate_columns = [keep.tile([P, T // P], F32, name=f"gate_columns{r}") for r in range(2)]
        with nc.allow_non_contiguous_dma(reason="one gate value a partition"):
            for r in (1, 0):
                nc.sync.dma_start(gate_columns[r][:], gate[r, 0, :].rearrange("(q p) -> p q", p=P))

        x_codes = keep.tile([P, T], U32, name="x_codes", tag="x_codes", align_bytes=64)
        for raw, (t0, t1) in zip(x_raw, pieces):
            x_bf = rounding.tile([P, t1 - t0, PACK], BF16, name="x_bf", align_bytes=64)
            source = raw[:].rearrange("p j (c i) -> p c j i", i=LINE)
            target = x_bf[:].rearrange("p (c i) j -> p c j i", i=LINE)
            share = (t1 - t0) * SCALAR_EIGHTHS // 8 // LINE
            middle = (t1 - t0) // 2
            nc.scalar.copy(target[:, :share], source[:, :share])
            nc.vector.tensor_copy(target[:, middle // LINE :], source[:, middle // LINE :])
            nc.vector.tensor_copy(target[:, share : middle // LINE], source[:, share : middle // LINE])
            for c0 in (middle, 0):
                tokens = slice(t0 + c0, t0 + c0 + middle)
                nc.vector.quantize_mx(
                    out=x_codes[:, tokens].bitcast(FP8X4),
                    scales=x_scales[:, tokens],
                    in_=x_bf[:, c0 : c0 + middle, :].rearrange("p t j -> p (t j)"),
                )

        slot_codes, slot_scales = {}, {}
        for cut, (s0, s1) in enumerate(zip(GATHER_CUTS[:-1], GATHER_CUTS[1:])):
            listed = offs_sb[:, s0 // LIST_ROWS : s1 // LIST_ROWS]
            scales = keep.tile([P, s1 - s0], U8, name=f"slot_scales{cut}", align_bytes=64)
            codes = keep.tile([P, s1 - s0], U32, name=f"slot_codes{cut}", align_bytes=64)
            nc.vector.tensor_copy(scales[:], x_scales[:].indirect(listed))
            nc.vector.tensor_copy(codes[:], x_codes[:].indirect(listed))
            for s in range(s0, s1, UNIT):
                slot_codes[s // UNIT] = codes[:, s - s0 : s - s0 + UNIT]
                slot_scales[s // UNIT] = scales[:, s - s0 : s - s0 + UNIT]

        h_codes = [keep.tile([P, C], U32, name=f"h_codes{e}", align_bytes=64) for e in range(E)]
        h_scales = [keep.tile([P, C], U8, name=f"h_scales{e}", align_bytes=64) for e in range(E)]
        a_banks, b_banks, act, hidden = {}, {}, {}, {}
        held = keep.tile([P, len(ON_GPSIMD), H], BF16, name="held", tag="x_codes", align_bytes=64)

        def first_product(banks, numbers, m, unit):
            e = unit // UNITS_PER_EXPERT
            banks[unit] = bank([P, H], numbers[unit])
            nc.tensor.matmul_mx(
                out=banks[unit][:],
                lhsT=slot_codes[unit].bitcast(FP8X4),
                lhsT_scale=slot_scales[unit],
                rhs=words[m][:, e, :].bitcast(FP4X4),
                rhs_scale=planes[m][:, e, :],
                start=True,
                stop=True,
            )

        def by_pair(sums):
            return sums[:].rearrange("s (p u d) -> s u p d", u=2, d=2)

        def paired(tile):
            return tile[:].rearrange("s (u p d) -> s u p d", u=2, d=2)

        def activate(unit):
            first_product(a_banks, A_BANKS, 0, unit)
            if unit == UNITS - 1:
                act[unit] = keep.tile([P, H], F32, name="act_last", tag="hidden_early")
            else:
                act[unit] = work.tile([P, H], F32, name="act")
            nc.scalar.activation(paired(act[unit]), by_pair(a_banks[unit]), SILU)

        def multiply(unit):
            first_product(b_banks, B_BANKS, 1, unit)
            if unit in ON_GPSIMD:
                up = work.tile([P, H], F32, name="up")
                nc.scalar.copy(paired(up), by_pair(b_banks[unit]))
                hidden[unit] = held[:, ON_GPSIMD.index(unit), :]
                nc.gpsimd.tensor_tensor(hidden[unit], act[unit][:], up[:], MULT)
            else:
                if unit == TURN_GROUPS[0][-1]:
                    hidden[unit] = keep.tile([P, H], BF16, name="hidden_early")
                elif unit == UNITS - 1:
                    hidden[unit] = keep.tile([P, H], BF16, name="hidden_late", tag="y_sb3", align_bytes=64)
                else:
                    hidden[unit] = work.tile([P, H], BF16, name="hidden")
                nc.vector.tensor_tensor(paired(hidden[unit]), paired(act[unit]), by_pair(b_banks[unit]), MULT)

        turned_by_group = {}

        def turn(group):
            units, number = TURN_GROUPS[group], TURN_BANKS[group]
            turned = bank([P, len(units), 2, UNIT], number)
            for n, unit in enumerate(units):
                pairs = hidden[unit][:].bitcast(F32)
                for u in range(2):
                    nc.tensor.transpose(turned[:, n, u, :], pairs[:, u * P : (u + 1) * P], ident[:])
            turned_by_group[group] = turned

        hidden_by_group = {}

        def turn_out(group):
            units, turned = TURN_GROUPS[group], turned_by_group[group]
            if group == len(TURN_GROUPS) - 1:
                hidden_k = late.tile([P, UNIT * PACK], BF16, name="hidden_last", align_bytes=64, offset=0)
            elif group == 2:
                hidden_k = late.tile([P, C * PACK], BF16, name="hidden_third", align_bytes=64, offset=4 * S)
            else:
                hidden_k = work.tile([P, len(units) * UNIT * PACK], BF16, name="hidden_k", align_bytes=64)
            nc.scalar.copy(
                hidden_k[:].bitcast(F32).rearrange("p (n s u) -> p n s u", u=2, s=UNIT),
                turned[:].rearrange("p n u s -> p n s u"),
            )
            hidden_by_group[group] = hidden_k

        def quantise(group):
            units, hidden_k = TURN_GROUPS[group], hidden_by_group[group]
            e, s0 = units[0] // UNITS_PER_EXPERT, units[0] % UNITS_PER_EXPERT * UNIT
            slots = slice(s0, s0 + len(units) * UNIT)
            nc.vector.quantize_mx(out=h_codes[e][:, slots].bitcast(FP8X4), scales=h_scales[e][:, slots], in_=hidden_k[:])

        for run in EARLY_RUNS:
            for stage in (activate, multiply):
                for unit in run:
                    stage(unit)
        third_last, second_last, last = range(UNITS - 3, UNITS)
        activate(third_last)
        activate(second_last)
        multiply(third_last)
        turn(0)
        turn_out(0)
        multiply(second_last)
        quantise(0)
        activate(last)
        multiply(last)
        for group in range(1, len(TURN_GROUPS)):
            turn(group)
        for group in range(1, len(TURN_GROUPS)):
            turn_out(group)
            quantise(group)

        y_sb = {}

        def second_product(target, b, e, c0, c1):
            nc.tensor.matmul_mx(
                out=target,
                lhsT=w2_sb[b][:, e, :].bitcast(FP4X4),
                lhsT_scale=planes[2][:, e, b * P : (b + 1) * P],
                rhs=h_codes[e][:, c0:c1].bitcast(FP8X4),
                rhs_scale=h_scales[e][:, c0:c1],
                start=True,
                stop=True,
            )

        def first_results():
            y_sb[0] = keep.tile([P, S], F32, name="y_sb0", align_bytes=64)
            for piece, (s0, s1) in enumerate(FIRST_PIECES):
                y_bank = bank([P, s1 - s0], TURN_BANKS[piece])
                e = s0 // C
                second_product(y_bank[:], 0, e, s0 - e * C, s1 - e * C)
                copy = nc.vector.tensor_copy if piece in FIRST_ON_VECTOR else nc.scalar.copy
                copy(y_sb[0][:, s0:s1], y_bank[:])
                if piece == 1:
                    later_results(3, 0, nc.scalar.copy)

        def later_results(b, piece, copy):
            if piece == 0 and b == 3:
                y_sb[b] = keep.tile([P, S], F32, name="y_sb3", align_bytes=64)
            elif piece == 0:
                y_sb[b] = late.tile([P, S], F32, name=f"y_sb{b}", align_bytes=64, offset=4 * S * (b - 1))
            experts = LATER_PIECES[b][piece]
            y_bank = bank([P, len(experts), C], LATER_BANKS[b][piece])
            low, high = min(experts), max(experts)
            for e in experts:
                second_product(y_bank[:, 0 if e == low else 1, :], b, e, 0, C)
            columns = slice(low, high + 1, max(1, high - low))
            copy(y_sb[b][:].rearrange("p (e c) -> p e c", c=C)[:, columns, :], y_bank[:])

        parts = {(b, r): work.tile([P, T], F32, name="part") for b in range(BLOCKS) for r in range(2)}
        picked = {}
        gate_rows = {}

        def spread_gate(r):
            gate_rows[r] = bank([P, T], GATE_BANKS[r])
            for q in range(T // P):
                nc.tensor.transpose(
                    gate_rows[r][:, q * P : (q + 1) * P], gate_columns[r][:, q : q + 1].to_broadcast([P, P]), ident[:]
                )

        def listed(r, t0, t1):
            return pos_sb[r][:, t0 // LIST_ROWS : t1 // LIST_ROWS]

        def pick_gated(b):
            nc.vector.tensor_tensor(parts[b, 0][:], y_sb[b][:].indirect(listed(0, 0, T)), first_gate[:], MULT)

        def pick(b, r, t0, t1):
            if t0 == 0:
                picked[b, r] = work.tile([P, T], F32, name="picked")
            nc.scalar.activation(picked[b, r][:, t0:t1], y_sb[b][:].indirect(listed(r, t0, t1)), COPY)

        def weigh(b, r, t0, t1):
            nc.vector.tensor_tensor(parts[b, r][:, t0:t1], picked[b, r][:, t0:t1], gate_rows[r][:, t0:t1], MULT)

        def add_and_store(engine, b, t0, t1):
            total = work.tile([P, t1 - t0], F32, name="total")
            engine.tensor_tensor(total[:], parts[b, 0][:, t0:t1], parts[b, 1][:, t0:t1], ADD)
            nc.sync.dma_start(out[b * P : (b + 1) * P, t0:t1], total[:])

        first_results()
        later_results(2, 0, nc.vector.tensor_copy)
        later_results(1, 0, nc.vector.tensor_copy)
        pick_gated(0)
        later_results(1, 1, nc.scalar.copy)
        pick_gated(1)
        spread_gate(1)
        pick(0, 1, 0, T)
        weigh(0, 1, 0, T)
        add_and_store(nc.gpsimd, 0, 0, T)
        later_results(2, 1, nc.scalar.copy)
        later_results(2, 2, nc.scalar.copy)
        pick_gated(2)
        later_results(3, 1, nc.vector.tensor_copy)
        pick(1, 1, 0, T)
        weigh(1, 1, 0, T)
        pick(2, 1, 0, T)
        weigh(2, 1, 0, T)
        add_and_store(nc.vector, 1, 0, T)
        add_and_store(nc.gpsimd, 2, 0, T)
        spread_gate(0)
        t0, t1, t2, t3 = LAST_CUTS
        pick(3, 0, t0, t1)
        pick(3, 1, t0, t1)
        pick(3, 0, t1, t3)
        pick(3, 1, t1, t2)
        pick(3, 1, t2, t3)
        weigh(3, 0, t0, t1)
        weigh(3, 1, t0, t1)
        weigh(3, 0, t1, t3)
        add_and_store(nc.vector, 3, t0, t1)
        weigh(3, 1, t1, t2)
        weigh(3, 1, t2, t3)
        add_and_store(nc.vector, 3, t1, t2)
        add_and_store(nc.vector, 3, t2, t3)
